import numpy as np
import ml_dtypes


def mxq(x, axis, fmt="e4m3"):
    dtype, down = {"e4m3": (ml_dtypes.float8_e4m3fn, 7), "e5m2": (ml_dtypes.float8_e5m2, 14)}[fmt]
    v = np.moveaxis(np.asarray(x, np.float32).astype(ml_dtypes.bfloat16).astype(np.float64), axis, -1)
    blocks = v.reshape(v.shape[:-1] + (-1, 32))
    amax = np.abs(blocks).max(-1, keepdims=True)
    byte = np.maximum(np.where(amax > 0, np.frexp(amax)[1] - 1 + 127, 0) - down, 1)
    scale = np.exp2(byte - 127.0)
    codes = (blocks / scale).astype(np.float32).astype(dtype).astype(np.float64)
    return np.moveaxis((codes * scale).reshape(v.shape), -1, axis)


WIDE = False


def mx_kscale(k):
    if not WIDE:
        return np.ones(k)
    levels = np.array([10, -10, 5, -5, 0])
    if k % 512:
        return np.exp2(np.random.permutation(np.resize(levels, k // 32))).repeat(32)
    a = np.empty((k // 512, 16))
    for p in range(k // 512):
        a[p, :8] = np.random.permutation(np.resize(levels, 8))
        for g in range(8):
            far = levels[np.abs(levels - a[p, g]) >= 10]
            a[p, g + 8] = far[np.random.randint(len(far))]
    return np.exp2(a.ravel()).repeat(32)


def f64(x):
    return np.asarray(x).astype(np.float64)


def striped(idx):
    return np.tile(idx.reshape(-1, 16).T, (8, 1)).astype(np.uint16)


def unstriped(offs):
    return offs[:16].T.reshape(-1).astype(np.int64)


def pack_weight(w):
    k, n = w.shape
    w = f64(np.asarray(w, np.float32).astype(ml_dtypes.bfloat16)).reshape(k // 32, 32, n)
    amax = np.abs(w).max(1)
    byte = np.clip(np.where(amax > 0, np.frexp(amax)[1] - 1 + 127 - 7, 1), 1, 254)
    scaled = (w * np.exp2(127.0 - byte)[:, None, :]).reshape(k, n).astype(np.float32)
    words = np.ascontiguousarray(scaled.reshape(k // 512, 128, 4, n).transpose(0, 1, 3, 2)).astype(ml_dtypes.float8_e4m3fn).view(np.uint8)
    return words, np.ascontiguousarray(byte.astype(np.uint8).reshape(k // 512, 16, n))


def unpack_weight(words, scales):
    g, p, n, _ = words.shape
    vals = np.ascontiguousarray(words).view(ml_dtypes.float8_e4m3fn).astype(np.float64) * np.repeat(np.exp2(scales.astype(np.float64) - 127.0), 8, axis=1)[..., None]
    return vals.transpose(0, 1, 3, 2).reshape(g * 512, n)


def relu(v):
    return np.maximum(v, 0.0)


K, T, S, V, N = 512, 2048, 512, 256, 128


def setup_inputs():
    n = np.random.standard_normal
    s = mx_kscale(K)[:, None]
    near = np.random.permutation(S)
    packed_xT = pack_weight(n((K, T)) * s)
    return {
        "x_words": packed_xT[0],
        "x_scales": packed_xT[1],
        "w1": (n((K, N)) / np.sqrt(K) / s).astype(np.float32),
        "w2": (n((K, N)) / np.sqrt(K) / s).astype(np.float32),
        "w3": (n((K, N)) / np.sqrt(K) / s).astype(np.float32),
        "pt": (n((N, V))).astype(np.float32),
        "offs": striped(np.random.permutation(T)[:S]),
        "pos1": striped(near[:V]),
        "pos2": striped(near[V:]),
        "pos3": striped(np.random.permutation(S)[:V]),
    }


def reference(x_words, x_scales, w1, w2, w3, pt, offs, pos1, pos2, pos3):
    xq = unpack_weight(x_words, x_scales)[:, unstriped(offs)]
    y = mxq(f64(w1), 0, "e4m3").T @ xq
    a = np.exp(mxq(f64(w3), 0, "e4m3").T @ xq)
    a0 = a[:, unstriped(pos1)]
    a1 = a[:, unstriped(pos2)]
    a2 = a[:, unstriped(pos3)]
    num = y[:, unstriped(pos1)] * a0 + y[:, unstriped(pos2)] * a1 + y[:, unstriped(pos3)] * a2
    den = a0 + a1 + a2
    cen = num / den
    dd = f64(pt) - cen
    rr = relu(mxq(f64(w2), 0, "e4m3").T @ xq)
    off = np.minimum(np.minimum(rr[:, unstriped(pos1)], rr[:, unstriped(pos2)]), rr[:, unstriped(pos3)])
    return relu(np.abs(dd) - off)

@@ -1,0 +1,180 @@
+from contextlib import ExitStack
+
+import concourse.mybir as mybir
+from concourse.masks import make_identity
+
+K, T, S, V, N = 512, 2048, 512, 256, 128
+FLOPS = 3 * 2 * K * N * S
+
+F32 = mybir.dt.float32
+BF16 = mybir.dt.bfloat16
+I32 = mybir.dt.int32
+U32 = mybir.dt.uint32
+U16 = mybir.dt.uint16
+U8 = mybir.dt.uint8
+FP8X4 = mybir.dt.float8_e4m3fn_x4
+ACT = mybir.ActivationFunctionType
+ALU = mybir.AluOpType
+
+P = 128
+PACK = 4
+HALF = S // 2
+BLOCKS = V // P
+
+
+def tile_picked_box_p_kernel(
+    tc, x_words, x_scales, w1, w2, w3, pt, offs, pos1, pos2, pos3, out
+):
+    nc = tc.nc
+    with ExitStack() as ctx:
+        keep = ctx.enter_context(tc.tile_pool(name="keep", bufs=1))
+        psum = ctx.enter_context(tc.psum_pool(name="psum", bufs=1))
+
+        def sb(name, shape, dtype, tag=None):
+            return keep.tile(shape, dtype, name=name, tag=tag or name, align_bytes=64)
+
+        def bank(name, tag):
+            return psum.tile([P, 512], F32, name=name, tag=tag)
+
+        def block(b):
+            return slice(b * P, (b + 1) * P)
+
+        scale_table = sb("scale_table", [P, T], U8)
+        nc.gpsimd.memset(scale_table[:].bitcast(I32), 0)
+        offs_sb = sb("offs_sb", [P, S // 16], U16)
+        nc.sync.dma_start(offs_sb[:], offs)
+        def load_weight(name, w, tag=None):
+            raw = sb(name + "_raw", [P, PACK, N], F32, tag)
+            nc.sync.dma_start(raw[:], w.rearrange("(p j) m -> p j m", j=PACK))
+            return raw
+
+        def load_list(i, pos):
+            tile = sb("pos%d_sb" % i, [P, V // 16], U16)
+            nc.sync.dma_start(tile[:], pos)
+            return tile
+
+        w3_raw = load_weight("w3", w3)
+        for q in range(4):
+            nc.sync.dma_start(
+                scale_table[32 * q : 32 * q + 4, :].bitcast(I32), x_scales[0, 4 * q : 4 * q + 4, :].bitcast(I32)
+            )
+
+        word_table = sb("word_table", [P, T], I32)
+        nc.sync.dma_start(word_table[:], x_words[0].rearrange("p n t -> p (n t)").bitcast(I32))
+        pos_sb = [load_list(i, pos) for i, pos in enumerate((pos1, pos2, pos3))]
+
+        ident = sb("ident", [P, P], F32)
+        make_identity(nc, ident[:])
+        warm = sb("warm", [P, 1], F32)
+        nc.scalar.activation(warm[:], ident[:, 0:1], ACT.Exp)
+
+        def interleave(name, raw, copy):
+            grouped = sb(name + "_grouped", [P, N, PACK], BF16)
+            copy(grouped[:], raw[:].rearrange("p j m -> p m j"))
+            return grouped
+
+        def quantize(name, grouped):
+            codes = sb(name + "_codes", [P, N], U32)
+            scales = sb(name + "_scales", [P, N], U8)
+            nc.vector.quantize_mx(
+                out=codes[:].bitcast(FP8X4), scales=scales[:], in_=grouped[:].rearrange("p m j -> p (m j)")
+            )
+            return codes, scales
+
+        x_scale = sb("x_scale", [P, S], U8)
+        x_code = sb("x_code", [P, S], U32)
+
+        def product(acc, weight, cols):
+            codes, scales = weight
+            nc.tensor.matmul_mx(
+                out=acc,
+                lhsT=codes[:].bitcast(FP8X4),
+                lhsT_scale=scales[:],
+                rhs=x_code[:, cols].bitcast(FP8X4),
+                rhs_scale=x_scale[:, cols],
+                start=True,
+                stop=True,
+            )
+
+        w3_grouped = interleave("w3", w3_raw, nc.vector.tensor_copy)
+        nc.vector.tensor_copy(x_scale[:], scale_table[:].indirect(offs_sb[:]))
+        w3_mx = quantize("w3", w3_grouped)
+        w1_raw = load_weight("w1", w1, "w3_raw")
+        w2_raw = load_weight("w2", w2, "w3_grouped")
+        pt_sb = sb("pt_sb", [P, V], F32, "scale_table")
+        nc.sync.dma_start(pt_sb[:], pt)
+
+        w1_grouped = interleave("w1", w1_raw, nc.scalar.copy)
+        a = sb("a", [P, S], F32, "w3_raw")
+        for h in range(2):
+            cols = slice(h * HALF, (h + 1) * HALF)
+            nc.vector.tensor_copy(
+                x_code[:, cols], word_table[:].bitcast(U32).indirect(offs_sb[:, h * HALF // 16 : (h + 1) * HALF // 16])
+            )
+            logits = bank("logits%d" % h, "logits%d" % h)
+            product(logits[:, :HALF], w3_mx, cols)
+            nc.scalar.activation(a[:, cols], logits[:, :HALF], ACT.Exp)
+
+        w1_mx = quantize("w1", w1_grouped)
+        y = bank("y", "y")
+        product(y[:], w1_mx, slice(0, S))
+        w2_mx = quantize("w2", interleave("w2", w2_raw, nc.vector.tensor_copy))
+        r = bank("r", "r")
+        product(r[:], w2_mx, slice(0, S))
+        rr = sb("rr", [P, S], F32)
+        nc.scalar.activation(rr[:], r[:], ACT.Relu)
+
+        def fetch(name, table, i, tag=None):
+            picked = sb("%s%d" % (name, i), [P, V], F32, tag)
+            nc.vector.tensor_copy(picked[:], table[:].indirect(pos_sb[i][:]))
+            return picked
+
+        def add_transposed(acc, terms):
+            for i, term in enumerate(terms):
+                nc.tensor.matmul(acc, term, ident[:], is_transpose=True, start=(i == 0), stop=(i == len(terms) - 1))
+
+        a_at = [fetch("a_at", a, 0, "w2_grouped")]
+        ya = sb("ya", [P, S], F32)
+        nc.vector.tensor_tensor(ya[:], y[:], a[:], ALU.mult)
+        a_at.extend(fetch("a_at", a, i) for i in (1, 2))
+
+        den_t = bank("den_t", "den_t")
+        for b in range(BLOCKS):
+            add_transposed(den_t[:, block(b)], [g[:, block(b)] for g in a_at])
+        root_t = sb("root_t", [P, V], F32)
+        nc.scalar.activation(root_t[:], den_t[:, :V], ACT.Abs_reciprocal_sqrt)
+        rec_t = [sb("rec_t%d" % b, [P, P], F32) for b in range(BLOCKS)]
+        for b in range(BLOCKS):
+            nc.scalar.activation(rec_t[b][:], root_t[:, block(b)], ACT.Square)
+
+        pt_t = bank("pt_t", "logits0")
+        for b in range(BLOCKS):
+            add_transposed(pt_t[:, block(b)], [pt_sb[:, block(b)]])
+        neg_pt_t = sb("neg_pt_t", [P, V], F32)
+        nc.scalar.activation(neg_pt_t[:], pt_t[:, :V], ACT.Copy, scale=-1.0)
+
+        ya_at = [fetch("ya_at", ya, i) for i in range(3)]
+        num_t = [bank("num_t0", "num_t0"), bank("num_t1", "logits1")]
+        for b in range(BLOCKS):
+            add_transposed(num_t[b][:, :P], [g[:, block(b)] for g in ya_at])
+
+        rr_at = [fetch("rr_at", rr, i) for i in range(2)]
+        cen_t = [sb("cen_t%d" % b, [P, P], F32) for b in range(BLOCKS)]
+        for b in range(BLOCKS):
+            nc.vector.tensor_tensor(cen_t[b][:], num_t[b][:, :P], rec_t[b][:], ALU.mult)
+        off01 = sb("off01", [P, V], F32, "rec_t0")
+        nc.vector.tensor_tensor(off01[:], rr_at[0][:], rr_at[1][:], ALU.min)
+        rr_at.append(fetch("rr_at", rr, 2, "rec_t1"))
+
+        dist = sb("dist", [P, V], F32)
+        for b in range(BLOCKS):
+            dd = bank("dd%d" % b, "dd%d" % b)
+            add_transposed(dd[:, :P], [neg_pt_t[:, block(b)], cen_t[b][:]])
+            nc.scalar.activation(dist[:, block(b)], dd[:, :P], ACT.Abs)
+        beyond01 = sb("beyond01", [P, V], F32)
+        nc.vector.tensor_tensor(beyond01[:], dist[:], off01[:], ALU.subtract)
+        beyond2 = sb("beyond2", [P, V], F32)
+        nc.vector.tensor_tensor(beyond2[:], dist[:], rr_at[2][:], ALU.subtract)
+        result = sb("result", [P, V], F32)
+        nc.vector.scalar_tensor_tensor(result[:], beyond01[:], 0.0, beyond2[:], ALU.max, ALU.max)
+        nc.sync.dma_start(out, result[:])

@@ -121,6 +121,8 @@ def tile_picked_box_p_kernel(
         w2_mx = quantize("w2", interleave("w2", w2_raw, nc.vector.tensor_copy))
         r = bank("r", "r")
         product(r[:], w2_mx, slice(0, S))
+        y_sb = sb("y_sb", [P, S], F32)
+        nc.scalar.activation(y_sb[:], y[:], ACT.Copy)
         rr = sb("rr", [P, S], F32)
         nc.scalar.activation(rr[:], r[:], ACT.Relu)
 
@@ -129,13 +131,16 @@ def tile_picked_box_p_kernel(
             nc.vector.tensor_copy(picked[:], table[:].indirect(pos_sb[i][:]))
             return picked
 
+        def fetch_with(name, table, i, other, op, tag=None):
+            picked = sb("%s%d" % (name, i), [P, V], F32, tag)
+            nc.vector.tensor_tensor(picked[:], table[:].indirect(pos_sb[i][:]), other[:], op)
+            return picked
+
         def add_transposed(acc, terms):
             for i, term in enumerate(terms):
                 nc.tensor.matmul(acc, term, ident[:], is_transpose=True, start=(i == 0), stop=(i == len(terms) - 1))
 
         a_at = [fetch("a_at", a, 0, "w2_grouped")]
-        ya = sb("ya", [P, S], F32)
-        nc.vector.tensor_tensor(ya[:], y[:], a[:], ALU.mult)
         a_at.extend(fetch("a_at", a, i) for i in (1, 2))
 
         den_t = bank("den_t", "den_t")
@@ -153,28 +158,30 @@ def tile_picked_box_p_kernel(
         neg_pt_t = sb("neg_pt_t", [P, V], F32)
         nc.scalar.activation(neg_pt_t[:], pt_t[:, :V], ACT.Copy, scale=-1.0)
 
-        ya_at = [fetch("ya_at", ya, i) for i in range(3)]
+        neg_rr = sb("neg_rr", [P, S], F32, "root_t")
+        nc.scalar.activation(neg_rr[:], rr[:], ACT.Copy, scale=-1.0)
+
+        ya_at = [fetch_with("ya_at", y_sb, i, a_at[i], ALU.mult) for i in range(3)]
         num_t = [bank("num_t0", "num_t0"), bank("num_t1", "logits1")]
         for b in range(BLOCKS):
             add_transposed(num_t[b][:, :P], [g[:, block(b)] for g in ya_at])
 
-        rr_at = [fetch("rr_at", rr, i) for i in range(2)]
+        rr0 = fetch("rr_at", rr, 0)
         cen_t = [sb("cen_t%d" % b, [P, P], F32) for b in range(BLOCKS)]
         for b in range(BLOCKS):
             nc.vector.tensor_tensor(cen_t[b][:], num_t[b][:, :P], rec_t[b][:], ALU.mult)
-        off01 = sb("off01", [P, V], F32, "rec_t0")
-        nc.vector.tensor_tensor(off01[:], rr_at[0][:], rr_at[1][:], ALU.min)
-        rr_at.append(fetch("rr_at", rr, 2, "rec_t1"))
+        rr1 = fetch("rr_at", rr, 1, "rec_t0")
+        off01 = sb("off01", [P, V], F32)
+        nc.vector.tensor_tensor(off01[:], rr0[:], rr1[:], ALU.min)
 
         dist = sb("dist", [P, V], F32)
         for b in range(BLOCKS):
             dd = bank("dd%d" % b, "dd%d" % b)
             add_transposed(dd[:, :P], [neg_pt_t[:, block(b)], cen_t[b][:]])
             nc.scalar.activation(dist[:, block(b)], dd[:, :P], ACT.Abs)
+        beyond2 = fetch_with("beyond", neg_rr, 2, dist, ALU.add)
         beyond01 = sb("beyond01", [P, V], F32)
         nc.vector.tensor_tensor(beyond01[:], dist[:], off01[:], ALU.subtract)
-        beyond2 = sb("beyond2", [P, V], F32)
-        nc.vector.tensor_tensor(beyond2[:], dist[:], rr_at[2][:], ALU.subtract)
         result = sb("result", [P, V], F32)
-        nc.vector.scalar_tensor_tensor(result[:], beyond01[:], 0.0, beyond2[:], ALU.max, ALU.max)
+        nc.vector.scalar_tensor_tensor(result[:], beyond2[:], 0.0, beyond01[:], ALU.max, ALU.max)
         nc.sync.dma_start(out, result[:])

@@ -54,10 +54,8 @@ def tile_picked_box_p_kernel(
             return tile
 
         w3_raw = load_weight("w3", w3)
-        for q in range(4):
-            nc.sync.dma_start(
-                scale_table[32 * q : 32 * q + 4, :].bitcast(I32), x_scales[0, 4 * q : 4 * q + 4, :].bitcast(I32)
-            )
+        for row in range(4):
+            nc.sync.dma_start(scale_table[row:P:32, :].bitcast(I32), x_scales[0, row:16:4, :].bitcast(I32))
 
         word_table = sb("word_table", [P, T], I32)
         nc.sync.dma_start(word_table[:], x_words[0].rearrange("p n t -> p (n t)").bitcast(I32))
@@ -111,9 +109,12 @@ def tile_picked_box_p_kernel(
             nc.vector.tensor_copy(
                 x_code[:, cols], word_table[:].bitcast(U32).indirect(offs_sb[:, h * HALF // 16 : (h + 1) * HALF // 16])
             )
-            logits = bank("logits%d" % h, "logits%d" % h)
-            product(logits[:, :HALF], w3_mx, cols)
-            nc.scalar.activation(a[:, cols], logits[:, :HALF], ACT.Exp)
+            pieces = [(cols, "logits0")] if h == 0 else [(slice(256, 384), "logits1"), (slice(384, 512), "dd0")]
+            for part, tag in pieces:
+                width = part.stop - part.start
+                logits = bank("logits_at%d" % part.start, tag)
+                product(logits[:, :width], w3_mx, part)
+                nc.scalar.activation(a[:, part], logits[:, :width], ACT.Exp)
 
         w1_mx = quantize("w1", w1_grouped)
         y = bank("y", "y")
@@ -180,8 +181,10 @@ def tile_picked_box_p_kernel(
             add_transposed(dd[:, :P], [neg_pt_t[:, block(b)], cen_t[b][:]])
             nc.scalar.activation(dist[:, block(b)], dd[:, :P], ACT.Abs)
         beyond2 = fetch_with("beyond", neg_rr, 2, dist, ALU.add)
-        beyond01 = sb("beyond01", [P, V], F32)
-        nc.vector.tensor_tensor(beyond01[:], dist[:], off01[:], ALU.subtract)
-        result = sb("result", [P, V], F32)
-        nc.vector.scalar_tensor_tensor(result[:], beyond2[:], 0.0, beyond01[:], ALU.max, ALU.max)
-        nc.sync.dma_start(out, result[:])
+        beyond01 = [sb("beyond01_%d" % b, [P, P], F32) for b in range(BLOCKS)]
+        for b in range(BLOCKS):
+            nc.vector.tensor_tensor(beyond01[b][:], dist[:, block(b)], off01[:, block(b)], ALU.subtract)
+        for b in range(BLOCKS):
+            result = sb("result%d" % b, [P, P], F32)
+            nc.vector.scalar_tensor_tensor(result[:], beyond2[:, block(b)], 0.0, beyond01[b][:], ALU.max, ALU.max)
+            nc.sync.dma_start(out[:, block(b)], result[:])

@@ -20,6 +20,7 @@ P = 128
 PACK = 4
 HALF = S // 2
 BLOCKS = V // P
+EARLY = T // 4
 
 
 def tile_picked_box_p_kernel(
@@ -54,11 +55,13 @@ def tile_picked_box_p_kernel(
             return tile
 
         w3_raw = load_weight("w3", w3)
+        word_table = sb("word_table", [P, T], I32)
+        words = x_words[0].rearrange("p n t -> p (n t)").bitcast(I32)
+        nc.sync.dma_start(word_table[:, :EARLY], words[:, :EARLY])
         for row in range(4):
             nc.sync.dma_start(scale_table[row:P:32, :].bitcast(I32), x_scales[0, row:16:4, :].bitcast(I32))
 
-        word_table = sb("word_table", [P, T], I32)
-        nc.sync.dma_start(word_table[:], x_words[0].rearrange("p n t -> p (n t)").bitcast(I32))
+        nc.sync.dma_start(word_table[:, EARLY:], words[:, EARLY:])
         pos_sb = [load_list(i, pos) for i, pos in enumerate((pos1, pos2, pos3))]
 
         ident = sb("ident", [P, P], F32)
@@ -95,8 +98,8 @@ def tile_picked_box_p_kernel(
             )
 
         w3_grouped = interleave("w3", w3_raw, nc.vector.tensor_copy)
-        nc.vector.tensor_copy(x_scale[:], scale_table[:].indirect(offs_sb[:]))
         w3_mx = quantize("w3", w3_grouped)
+        nc.vector.tensor_copy(x_scale[:], scale_table[:].indirect(offs_sb[:]))
         w1_raw = load_weight("w1", w1, "w3_raw")
         w2_raw = load_weight("w2", w2, "w3_grouped")
         pt_sb = sb("pt_sb", [P, V], F32, "scale_table")
@@ -116,10 +119,11 @@ def tile_picked_box_p_kernel(
                 product(logits[:, :width], w3_mx, part)
                 nc.scalar.activation(a[:, part], logits[:, :width], ACT.Exp)
 
+        w2_grouped = interleave("w2", w2_raw, nc.vector.tensor_copy)
         w1_mx = quantize("w1", w1_grouped)
         y = bank("y", "y")
         product(y[:], w1_mx, slice(0, S))
-        w2_mx = quantize("w2", interleave("w2", w2_raw, nc.vector.tensor_copy))
+        w2_mx = quantize("w2", w2_grouped)
         r = bank("r", "r")
         product(r[:], w2_mx, slice(0, S))
         y_sb = sb("y_sb", [P, S], F32)
@@ -164,8 +168,11 @@ def tile_picked_box_p_kernel(
 
         ya_at = [fetch_with("ya_at", y_sb, i, a_at[i], ALU.mult) for i in range(3)]
         num_t = [bank("num_t0", "num_t0"), bank("num_t1", "logits1")]
-        for b in range(BLOCKS):
-            add_transposed(num_t[b][:, :P], [g[:, block(b)] for g in ya_at])
+        for i, g in enumerate(ya_at):
+            for b in range(BLOCKS):
+                nc.tensor.matmul(
+                    num_t[b][:, :P], g[:, block(b)], ident[:], is_transpose=True, start=(i == 0), stop=(i == 2)
+                )
 
         rr0 = fetch("rr_at", rr, 0)
         cen_t = [sb("cen_t%d" % b, [P, P], F32) for b in range(BLOCKS)]
@@ -184,7 +191,9 @@ def tile_picked_box_p_kernel(
         beyond01 = [sb("beyond01_%d" % b, [P, P], F32) for b in range(BLOCKS)]
         for b in range(BLOCKS):
             nc.vector.tensor_tensor(beyond01[b][:], dist[:, block(b)], off01[:, block(b)], ALU.subtract)
+        result = sb("result", [P, V], F32)
         for b in range(BLOCKS):
-            result = sb("result%d" % b, [P, P], F32)
-            nc.vector.scalar_tensor_tensor(result[:], beyond2[:, block(b)], 0.0, beyond01[b][:], ALU.max, ALU.max)
-            nc.sync.dma_start(out[:, block(b)], result[:])
+            nc.vector.scalar_tensor_tensor(
+                result[:, block(b)], beyond2[:, block(b)], 0.0, beyond01[b][:], ALU.max, ALU.max
+            )
+        nc.sync.dma_start(out, result[:])

@@ -63,6 +63,8 @@ def tile_picked_box_p_kernel(
 
         nc.sync.dma_start(word_table[:, EARLY:], words[:, EARLY:])
         pos_sb = [load_list(i, pos) for i, pos in enumerate((pos1, pos2, pos3))]
+        w1_raw = load_weight("w1", w1)
+        w2_raw = load_weight("w2", w2)
 
         ident = sb("ident", [P, P], F32)
         make_identity(nc, ident[:])
@@ -100,19 +102,17 @@ def tile_picked_box_p_kernel(
         w3_grouped = interleave("w3", w3_raw, nc.vector.tensor_copy)
         w3_mx = quantize("w3", w3_grouped)
         nc.vector.tensor_copy(x_scale[:], scale_table[:].indirect(offs_sb[:]))
-        w1_raw = load_weight("w1", w1, "w3_raw")
-        w2_raw = load_weight("w2", w2, "w3_grouped")
         pt_sb = sb("pt_sb", [P, V], F32, "scale_table")
         nc.sync.dma_start(pt_sb[:], pt)
 
         w1_grouped = interleave("w1", w1_raw, nc.scalar.copy)
-        a = sb("a", [P, S], F32, "w3_raw")
+        a = sb("a", [P, S], F32, "w1_raw")
         for h in range(2):
             cols = slice(h * HALF, (h + 1) * HALF)
             nc.vector.tensor_copy(
                 x_code[:, cols], word_table[:].bitcast(U32).indirect(offs_sb[:, h * HALF // 16 : (h + 1) * HALF // 16])
             )
-            pieces = [(cols, "logits0")] if h == 0 else [(slice(256, 384), "logits1"), (slice(384, 512), "dd0")]
+            pieces = [(cols, "logits0")] if h == 0 else [(slice(256, 384), "logits1"), (slice(384, 512), "logits2")]
             for part, tag in pieces:
                 width = part.stop - part.start
                 logits = bank("logits_at%d" % part.start, tag)
@@ -121,73 +121,90 @@ def tile_picked_box_p_kernel(
 
         w2_grouped = interleave("w2", w2_raw, nc.vector.tensor_copy)
         w1_mx = quantize("w1", w1_grouped)
-        y = bank("y", "y")
-        product(y[:], w1_mx, slice(0, S))
-        w2_mx = quantize("w2", w2_grouped)
-        r = bank("r", "r")
-        product(r[:], w2_mx, slice(0, S))
         y_sb = sb("y_sb", [P, S], F32)
-        nc.scalar.activation(y_sb[:], y[:], ACT.Copy)
+        for h in range(2):
+            cols = slice(h * HALF, (h + 1) * HALF)
+            y = bank("y%d" % h, "y%d" % h)
+            product(y[:, :HALF], w1_mx, cols)
+            nc.scalar.activation(y_sb[:, cols], y[:, :HALF], ACT.Copy)
+        w2_mx = quantize("w2", w2_grouped)
         rr = sb("rr", [P, S], F32)
-        nc.scalar.activation(rr[:], r[:], ACT.Relu)
+        for h in range(2):
+            cols = slice(h * HALF, (h + 1) * HALF)
+            r = bank("r%d" % h, "r%d" % h)
+            product(r[:, :HALF], w2_mx, cols)
+            nc.scalar.activation(rr[:, cols], r[:, :HALF], ACT.Relu)
 
-        def fetch(name, table, i, tag=None):
+        def pieces_of(i, count):
+            width = V // count
+            return [
+                (slice(c * width, (c + 1) * width), pos_sb[i][:, c * width // 16 : (c + 1) * width // 16])
+                for c in range(count)
+            ]
+
+        def fetch(name, table, i, tag=None, count=1):
             picked = sb("%s%d" % (name, i), [P, V], F32, tag)
-            nc.vector.tensor_copy(picked[:], table[:].indirect(pos_sb[i][:]))
+            for cols, offsets in pieces_of(i, count):
+                nc.vector.tensor_copy(picked[:, cols], table[:].indirect(offsets))
             return picked
 
-        def fetch_with(name, table, i, other, op, tag=None):
-            picked = sb("%s%d" % (name, i), [P, V], F32, tag)
-            nc.vector.tensor_tensor(picked[:], table[:].indirect(pos_sb[i][:]), other[:], op)
+        def fetch_with(name, table, i, other, op, count=1):
+            picked = sb("%s%d" % (name, i), [P, V], F32)
+            for cols, offsets in pieces_of(i, count):
+                nc.vector.tensor_tensor(picked[:, cols], table[:].indirect(offsets), other[:, cols], op)
             return picked
 
         def add_transposed(acc, terms):
             for i, term in enumerate(terms):
                 nc.tensor.matmul(acc, term, ident[:], is_transpose=True, start=(i == 0), stop=(i == len(terms) - 1))
 
+        def add_lists(banks, picked):
+            for i, g in enumerate(picked):
+                for b in range(BLOCKS):
+                    nc.tensor.matmul(
+                        banks[b][:, :P], g[:, block(b)], ident[:], is_transpose=True, start=(i == 0), stop=(i == 2)
+                    )
+
         a_at = [fetch("a_at", a, 0, "w2_grouped")]
         a_at.extend(fetch("a_at", a, i) for i in (1, 2))
 
-        den_t = bank("den_t", "den_t")
+        den_t = [bank("den_t%d" % b, "logits%d" % b) for b in range(BLOCKS)]
+        add_lists(den_t, a_at)
+        root_t = [sb("root_t%d" % b, [P, P], F32) for b in range(BLOCKS)]
         for b in range(BLOCKS):
-            add_transposed(den_t[:, block(b)], [g[:, block(b)] for g in a_at])
-        root_t = sb("root_t", [P, V], F32)
-        nc.scalar.activation(root_t[:], den_t[:, :V], ACT.Abs_reciprocal_sqrt)
+            nc.scalar.activation(root_t[b][:], den_t[b][:, :P], ACT.Abs_reciprocal_sqrt)
         rec_t = [sb("rec_t%d" % b, [P, P], F32) for b in range(BLOCKS)]
         for b in range(BLOCKS):
-            nc.scalar.activation(rec_t[b][:], root_t[:, block(b)], ACT.Square)
+            nc.scalar.activation(rec_t[b][:], root_t[b][:], ACT.Square)
 
-        pt_t = bank("pt_t", "logits0")
+        pt_t = bank("pt_t", "r0")
         for b in range(BLOCKS):
             add_transposed(pt_t[:, block(b)], [pt_sb[:, block(b)]])
-        neg_pt_t = sb("neg_pt_t", [P, V], F32)
+        neg_pt_t = sb("neg_pt_t", [P, V], F32, "root_t0")
         nc.scalar.activation(neg_pt_t[:], pt_t[:, :V], ACT.Copy, scale=-1.0)
 
-        neg_rr = sb("neg_rr", [P, S], F32, "root_t")
+        neg_rr = sb("neg_rr", [P, S], F32, "root_t1")
         nc.scalar.activation(neg_rr[:], rr[:], ACT.Copy, scale=-1.0)
 
-        ya_at = [fetch_with("ya_at", y_sb, i, a_at[i], ALU.mult) for i in range(3)]
-        num_t = [bank("num_t0", "num_t0"), bank("num_t1", "logits1")]
-        for i, g in enumerate(ya_at):
-            for b in range(BLOCKS):
-                nc.tensor.matmul(
-                    num_t[b][:, :P], g[:, block(b)], ident[:], is_transpose=True, start=(i == 0), stop=(i == 2)
-                )
+        ya_at = [fetch_with("ya_at", y_sb, i, a_at[i], ALU.mult, BLOCKS if i == 2 else 1) for i in range(3)]
+        num_t = [bank("num_t%d" % b, "y%d" % b) for b in range(BLOCKS)]
+        add_lists(num_t, ya_at)
 
         rr0 = fetch("rr_at", rr, 0)
         cen_t = [sb("cen_t%d" % b, [P, P], F32) for b in range(BLOCKS)]
         for b in range(BLOCKS):
             nc.vector.tensor_tensor(cen_t[b][:], num_t[b][:, :P], rec_t[b][:], ALU.mult)
-        rr1 = fetch("rr_at", rr, 1, "rec_t0")
+        rr1 = fetch("rr_at", rr, 1, "rec_t0", BLOCKS)
         off01 = sb("off01", [P, V], F32)
-        nc.vector.tensor_tensor(off01[:], rr0[:], rr1[:], ALU.min)
+        for b in range(BLOCKS):
+            nc.vector.tensor_tensor(off01[:, block(b)], rr0[:, block(b)], rr1[:, block(b)], ALU.min)
 
         dist = sb("dist", [P, V], F32)
         for b in range(BLOCKS):
-            dd = bank("dd%d" % b, "dd%d" % b)
-            add_transposed(dd[:, :P], [neg_pt_t[:, block(b)], cen_t[b][:]])
+            dd = bank("dd%d" % b, ("logits2", "r1")[b])
+            add_transposed(dd[:, :P], [cen_t[b][:], neg_pt_t[:, block(b)]])
             nc.scalar.activation(dist[:, block(b)], dd[:, :P], ACT.Abs)
-        beyond2 = fetch_with("beyond", neg_rr, 2, dist, ALU.add)
+        beyond2 = fetch_with("beyond", neg_rr, 2, dist, ALU.add, BLOCKS)
         beyond01 = [sb("beyond01_%d" % b, [P, P], F32) for b in range(BLOCKS)]
         for b in range(BLOCKS):
             nc.vector.tensor_tensor(beyond01[b][:], dist[:, block(b)], off01[:, block(b)], ALU.subtract)

@@ -20,7 +20,6 @@ P = 128
 PACK = 4
 HALF = S // 2
 BLOCKS = V // P
-EARLY = T // 4
 
 
 def tile_picked_box_p_kernel(
@@ -55,13 +54,11 @@ def tile_picked_box_p_kernel(
             return tile
 
         w3_raw = load_weight("w3", w3)
-        word_table = sb("word_table", [P, T], I32)
-        words = x_words[0].rearrange("p n t -> p (n t)").bitcast(I32)
-        nc.sync.dma_start(word_table[:, :EARLY], words[:, :EARLY])
         for row in range(4):
             nc.sync.dma_start(scale_table[row:P:32, :].bitcast(I32), x_scales[0, row:16:4, :].bitcast(I32))
 
-        nc.sync.dma_start(word_table[:, EARLY:], words[:, EARLY:])
+        word_table = sb("word_table", [P, T], I32)
+        nc.sync.dma_start(word_table[:], x_words[0].rearrange("p n t -> p (n t)").bitcast(I32))
         pos_sb = [load_list(i, pos) for i, pos in enumerate((pos1, pos2, pos3))]
         w1_raw = load_weight("w1", w1)
         w2_raw = load_weight("w2", w2)
@@ -165,8 +162,7 @@ def tile_picked_box_p_kernel(
                         banks[b][:, :P], g[:, block(b)], ident[:], is_transpose=True, start=(i == 0), stop=(i == 2)
                     )
 
-        a_at = [fetch("a_at", a, 0, "w2_grouped")]
-        a_at.extend(fetch("a_at", a, i) for i in (1, 2))
+        a_at = [fetch("a_at", a, i) for i in range(3)]
 
         den_t = [bank("den_t%d" % b, "logits%d" % b) for b in range(BLOCKS)]
         add_lists(den_t, a_at)

@@ -59,8 +59,8 @@ def tile_picked_box_p_kernel(
 
         word_table = sb("word_table", [P, T], I32)
         nc.sync.dma_start(word_table[:], x_words[0].rearrange("p n t -> p (n t)").bitcast(I32))
-        pos_sb = [load_list(i, pos) for i, pos in enumerate((pos1, pos2, pos3))]
         w1_raw = load_weight("w1", w1)
+        pos_sb = [load_list(i, pos) for i, pos in enumerate((pos1, pos2, pos3))]
         w2_raw = load_weight("w2", w2)
 
         ident = sb("ident", [P, P], F32)
@@ -70,7 +70,10 @@ def tile_picked_box_p_kernel(
 
         def interleave(name, raw, copy):
             grouped = sb(name + "_grouped", [P, N, PACK], BF16)
-            copy(grouped[:], raw[:].rearrange("p j m -> p m j"))
+            copy(
+                grouped[:].rearrange("p (c i) j -> p c j i", i=4),
+                raw[:].rearrange("p j (c i) -> p c j i", i=4),
+            )
             return grouped
 
         def quantize(name, grouped):
@@ -116,8 +119,8 @@ def tile_picked_box_p_kernel(
                 product(logits[:, :width], w3_mx, part)
                 nc.scalar.activation(a[:, part], logits[:, :width], ACT.Exp)
 
-        w2_grouped = interleave("w2", w2_raw, nc.vector.tensor_copy)
         w1_mx = quantize("w1", w1_grouped)
+        w2_grouped = interleave("w2", w2_raw, nc.vector.tensor_copy)
         y_sb = sb("y_sb", [P, S], F32)
         for h in range(2):
             cols = slice(h * HALF, (h + 1) * HALF)

@@ -39,8 +39,11 @@ def tile_picked_box_p_kernel(
         def block(b):
             return slice(b * P, (b + 1) * P)
 
+        zero = sb("zero", [P, 1], F32)
+        nc.gpsimd.memset(zero[:], 0.0)
         scale_table = sb("scale_table", [P, T], U8)
-        nc.gpsimd.memset(scale_table[:].bitcast(I32), 0)
+        nc.gpsimd.memset(scale_table[0:48, :].bitcast(I32), 0)
+        nc.gpsimd.memset(scale_table[64:P, :].bitcast(I32), 0)
         offs_sb = sb("offs_sb", [P, S // 16], U16)
         nc.sync.dma_start(offs_sb[:], offs)
         def load_weight(name, w, tag=None):
@@ -53,39 +56,37 @@ def tile_picked_box_p_kernel(
             nc.sync.dma_start(tile[:], pos)
             return tile
 
+        nc.sync.dma_start(scale_table[48:64, :].bitcast(I32), x_scales[0].bitcast(I32))
         w3_raw = load_weight("w3", w3)
-        for row in range(4):
-            nc.sync.dma_start(scale_table[row:P:32, :].bitcast(I32), x_scales[0, row:16:4, :].bitcast(I32))
+        pos_sb = [load_list(i, pos) for i, pos in enumerate((pos1, pos2, pos3))]
 
         word_table = sb("word_table", [P, T], I32)
         nc.sync.dma_start(word_table[:], x_words[0].rearrange("p n t -> p (n t)").bitcast(I32))
         w1_raw = load_weight("w1", w1)
-        pos_sb = [load_list(i, pos) for i, pos in enumerate((pos1, pos2, pos3))]
-        w2_raw = load_weight("w2", w2)
 
+        x_scale = sb("x_scale", [P, S], U8)
+        nc.gpsimd.memset(x_scale[:].bitcast(I32), 0)
         ident = sb("ident", [P, P], F32)
         make_identity(nc, ident[:])
         warm = sb("warm", [P, 1], F32)
-        nc.scalar.activation(warm[:], ident[:, 0:1], ACT.Exp)
+        nc.scalar.activation(warm[:], zero[:], ACT.Exp)
 
-        def interleave(name, raw, copy):
-            grouped = sb(name + "_grouped", [P, N, PACK], BF16)
+        def interleave(name, raw, copy, tag=None):
+            grouped = sb(name + "_grouped", [P, N, PACK], BF16, tag)
             copy(
                 grouped[:].rearrange("p (c i) j -> p c j i", i=4),
                 raw[:].rearrange("p j (c i) -> p c j i", i=4),
             )
             return grouped
 
-        def quantize(name, grouped):
-            codes = sb(name + "_codes", [P, N], U32)
+        def quantize(name, grouped, tag=None):
+            codes = sb(name + "_codes", [P, N], U32, tag)
             scales = sb(name + "_scales", [P, N], U8)
             nc.vector.quantize_mx(
                 out=codes[:].bitcast(FP8X4), scales=scales[:], in_=grouped[:].rearrange("p m j -> p (m j)")
             )
             return codes, scales
 
-        x_scale = sb("x_scale", [P, S], U8)
-        x_code = sb("x_code", [P, S], U32)
 
         def product(acc, weight, cols):
             codes, scales = weight
@@ -99,12 +100,17 @@ def tile_picked_box_p_kernel(
                 stop=True,
             )
 
-        w3_grouped = interleave("w3", w3_raw, nc.vector.tensor_copy)
+        scale_picked = sb("scale_picked", [P, S], U8)
+        nc.vector.tensor_copy(scale_picked[:], scale_table[:].indirect(offs_sb[:]))
+        w3_grouped = interleave("w3", w3_raw, nc.vector.tensor_copy, "scale_table")
         w3_mx = quantize("w3", w3_grouped)
-        nc.vector.tensor_copy(x_scale[:], scale_table[:].indirect(offs_sb[:]))
-        pt_sb = sb("pt_sb", [P, V], F32, "scale_table")
-        nc.sync.dma_start(pt_sb[:], pt)
+        w2_raw = load_weight("w2", w2, "w3_raw")
+        x_code = sb("x_code", [P, S], U32, "scale_table")
+        for j in range(4):
+            nc.scalar.dma_start(x_scale[j:P:32, :].bitcast(I32), scale_picked[48 + j : 64 : 4, :].bitcast(I32))
 
+        pt_sb = sb("pt_sb", [P, V], F32, "scale_picked")
+        nc.sync.dma_start(pt_sb[:], pt)
         w1_grouped = interleave("w1", w1_raw, nc.scalar.copy)
         a = sb("a", [P, S], F32, "w1_raw")
         for h in range(2):

@@ -118,7 +118,7 @@ def tile_picked_box_p_kernel(
             nc.vector.tensor_copy(
                 x_code[:, cols], word_table[:].bitcast(U32).indirect(offs_sb[:, h * HALF // 16 : (h + 1) * HALF // 16])
             )
-            pieces = [(cols, "logits0")] if h == 0 else [(slice(256, 384), "logits1"), (slice(384, 512), "logits2")]
+            pieces = [(block(2 * h + c), "logits%d" % (2 * h + c)) for c in range(2)]
             for part, tag in pieces:
                 width = part.stop - part.start
                 logits = bank("logits_at%d" % part.start, tag)

@@ -207,11 +207,12 @@ def tile_picked_box_p_kernel(
         dist = sb("dist", [P, V], F32)
         for b in range(BLOCKS):
             dd = bank("dd%d" % b, ("logits2", "r1")[b])
-            add_transposed(dd[:, :P], [cen_t[b][:], neg_pt_t[:, block(b)]])
+            add_transposed(dd[:, :P], [neg_pt_t[:, block(b)], cen_t[b][:]])
             nc.scalar.activation(dist[:, block(b)], dd[:, :P], ACT.Abs)
-        beyond2 = fetch_with("beyond", neg_rr, 2, dist, ALU.add, BLOCKS)
+        beyond2 = sb("beyond2", [P, V], F32)
         beyond01 = [sb("beyond01_%d" % b, [P, P], F32) for b in range(BLOCKS)]
-        for b in range(BLOCKS):
+        for b, (cols, offsets) in enumerate(pieces_of(2, BLOCKS)):
+            nc.vector.tensor_tensor(beyond2[:, cols], neg_rr[:].indirect(offsets), dist[:, cols], ALU.add)
             nc.vector.tensor_tensor(beyond01[b][:], dist[:, block(b)], off01[:, block(b)], ALU.subtract)
         result = sb("result", [P, V], F32)
         for b in range(BLOCKS):

@@ -18,8 +18,16 @@ ALU = mybir.AluOpType
 
 P = 128
 PACK = 4
+RUN = 4
+GROUP = 16
+QUADRANT = 32
+ROWS = 4
+BANK = 512
+LISTS = 3
 HALF = S // 2
 BLOCKS = V // P
+STAGE_END = P // 2
+STAGE = STAGE_END - K // QUADRANT
 
 
 def tile_picked_box_p_kernel(
@@ -34,59 +42,42 @@ def tile_picked_box_p_kernel(
             return keep.tile(shape, dtype, name=name, tag=tag or name, align_bytes=64)
 
         def bank(name, tag):
-            return psum.tile([P, 512], F32, name=name, tag=tag)
+            return psum.tile([P, BANK], F32, name=name, tag=tag)
 
         def block(b):
             return slice(b * P, (b + 1) * P)
 
-        zero = sb("zero", [P, 1], F32)
-        nc.gpsimd.memset(zero[:], 0.0)
-        scale_table = sb("scale_table", [P, T], U8)
-        nc.gpsimd.memset(scale_table[0:48, :].bitcast(I32), 0)
-        nc.gpsimd.memset(scale_table[64:P, :].bitcast(I32), 0)
-        offs_sb = sb("offs_sb", [P, S // 16], U16)
-        nc.sync.dma_start(offs_sb[:], offs)
+        def half(h):
+            return slice(h * HALF, (h + 1) * HALF)
+
+        def entries(list_tile, cols):
+            return list_tile[:, cols.start // GROUP : cols.stop // GROUP]
+
         def load_weight(name, w, tag=None):
             raw = sb(name + "_raw", [P, PACK, N], F32, tag)
             nc.sync.dma_start(raw[:], w.rearrange("(p j) m -> p j m", j=PACK))
             return raw
 
         def load_list(i, pos):
-            tile = sb("pos%d_sb" % i, [P, V // 16], U16)
+            tile = sb("pos%d_sb" % i, [P, V // GROUP], U16)
             nc.sync.dma_start(tile[:], pos)
             return tile
-
-        nc.sync.dma_start(scale_table[48:64, :].bitcast(I32), x_scales[0].bitcast(I32))
-        w3_raw = load_weight("w3", w3)
-        pos_sb = [load_list(i, pos) for i, pos in enumerate((pos1, pos2, pos3))]
-
-        word_table = sb("word_table", [P, T], I32)
-        nc.sync.dma_start(word_table[:], x_words[0].rearrange("p n t -> p (n t)").bitcast(I32))
-        w1_raw = load_weight("w1", w1)
-
-        x_scale = sb("x_scale", [P, S], U8)
-        nc.gpsimd.memset(x_scale[:].bitcast(I32), 0)
-        ident = sb("ident", [P, P], F32)
-        make_identity(nc, ident[:])
-        warm = sb("warm", [P, 1], F32)
-        nc.scalar.activation(warm[:], zero[:], ACT.Exp)
 
         def interleave(name, raw, copy, tag=None):
             grouped = sb(name + "_grouped", [P, N, PACK], BF16, tag)
             copy(
-                grouped[:].rearrange("p (c i) j -> p c j i", i=4),
-                raw[:].rearrange("p j (c i) -> p c j i", i=4),
+                grouped[:].rearrange("p (c i) j -> p c j i", i=RUN),
+                raw[:].rearrange("p j (c i) -> p c j i", i=RUN),
             )
             return grouped
 
-        def quantize(name, grouped, tag=None):
-            codes = sb(name + "_codes", [P, N], U32, tag)
+        def quantize(name, grouped):
+            codes = sb(name + "_codes", [P, N], U32)
             scales = sb(name + "_scales", [P, N], U8)
             nc.vector.quantize_mx(
                 out=codes[:].bitcast(FP8X4), scales=scales[:], in_=grouped[:].rearrange("p m j -> p (m j)")
             )
             return codes, scales
-
 
         def product(acc, weight, cols):
             codes, scales = weight
@@ -100,64 +91,22 @@ def tile_picked_box_p_kernel(
                 stop=True,
             )
 
-        scale_picked = sb("scale_picked", [P, S], U8)
-        nc.vector.tensor_copy(scale_picked[:], scale_table[:].indirect(offs_sb[:]))
-        w3_grouped = interleave("w3", w3_raw, nc.vector.tensor_copy, "scale_table")
-        w3_mx = quantize("w3", w3_grouped)
-        w2_raw = load_weight("w2", w2, "w3_raw")
-        x_code = sb("x_code", [P, S], U32, "scale_table")
-        for j in range(4):
-            nc.scalar.dma_start(x_scale[j:P:32, :].bitcast(I32), scale_picked[48 + j : 64 : 4, :].bitcast(I32))
-
-        pt_sb = sb("pt_sb", [P, V], F32, "scale_picked")
-        nc.sync.dma_start(pt_sb[:], pt)
-        w1_grouped = interleave("w1", w1_raw, nc.scalar.copy)
-        a = sb("a", [P, S], F32, "w1_raw")
-        for h in range(2):
-            cols = slice(h * HALF, (h + 1) * HALF)
-            nc.vector.tensor_copy(
-                x_code[:, cols], word_table[:].bitcast(U32).indirect(offs_sb[:, h * HALF // 16 : (h + 1) * HALF // 16])
-            )
-            pieces = [(block(2 * h + c), "logits%d" % (2 * h + c)) for c in range(2)]
-            for part, tag in pieces:
-                width = part.stop - part.start
-                logits = bank("logits_at%d" % part.start, tag)
-                product(logits[:, :width], w3_mx, part)
-                nc.scalar.activation(a[:, part], logits[:, :width], ACT.Exp)
-
-        w1_mx = quantize("w1", w1_grouped)
-        w2_grouped = interleave("w2", w2_raw, nc.vector.tensor_copy)
-        y_sb = sb("y_sb", [P, S], F32)
-        for h in range(2):
-            cols = slice(h * HALF, (h + 1) * HALF)
-            y = bank("y%d" % h, "y%d" % h)
-            product(y[:, :HALF], w1_mx, cols)
-            nc.scalar.activation(y_sb[:, cols], y[:, :HALF], ACT.Copy)
-        w2_mx = quantize("w2", w2_grouped)
-        rr = sb("rr", [P, S], F32)
-        for h in range(2):
-            cols = slice(h * HALF, (h + 1) * HALF)
-            r = bank("r%d" % h, "r%d" % h)
-            product(r[:, :HALF], w2_mx, cols)
-            nc.scalar.activation(rr[:, cols], r[:, :HALF], ACT.Relu)
-
-        def pieces_of(i, count):
+        def pieces(count):
             width = V // count
-            return [
-                (slice(c * width, (c + 1) * width), pos_sb[i][:, c * width // 16 : (c + 1) * width // 16])
-                for c in range(count)
-            ]
+            return [slice(c * width, (c + 1) * width) for c in range(count)]
 
         def fetch(name, table, i, tag=None, count=1):
             picked = sb("%s%d" % (name, i), [P, V], F32, tag)
-            for cols, offsets in pieces_of(i, count):
-                nc.vector.tensor_copy(picked[:, cols], table[:].indirect(offsets))
+            for cols in pieces(count):
+                nc.vector.tensor_copy(picked[:, cols], table[:].indirect(entries(pos_sb[i], cols)))
             return picked
 
-        def fetch_with(name, table, i, other, op, count=1):
+        def fetch_times(name, table, i, factor, count):
             picked = sb("%s%d" % (name, i), [P, V], F32)
-            for cols, offsets in pieces_of(i, count):
-                nc.vector.tensor_tensor(picked[:, cols], table[:].indirect(offsets), other[:, cols], op)
+            for cols in pieces(count):
+                nc.vector.tensor_tensor(
+                    picked[:, cols], table[:].indirect(entries(pos_sb[i], cols)), factor[:, cols], ALU.mult
+                )
             return picked
 
         def add_transposed(acc, terms):
@@ -165,14 +114,76 @@ def tile_picked_box_p_kernel(
                 nc.tensor.matmul(acc, term, ident[:], is_transpose=True, start=(i == 0), stop=(i == len(terms) - 1))
 
         def add_lists(banks, picked):
-            for i, g in enumerate(picked):
+            for i, term in enumerate(picked):
                 for b in range(BLOCKS):
                     nc.tensor.matmul(
-                        banks[b][:, :P], g[:, block(b)], ident[:], is_transpose=True, start=(i == 0), stop=(i == 2)
+                        banks[b][:, :P],
+                        term[:, block(b)],
+                        ident[:],
+                        is_transpose=True,
+                        start=(i == 0),
+                        stop=(i == LISTS - 1),
                     )
 
-        a_at = [fetch("a_at", a, i) for i in range(3)]
+        zero = sb("zero", [P, 1], F32)
+        nc.gpsimd.memset(zero[:], 0.0)
 
+        scale_table = sb("scale_table", [P, T], U8)
+        nc.gpsimd.memset(scale_table[0:STAGE, :].bitcast(I32), 0)
+        nc.gpsimd.memset(scale_table[STAGE_END:P, :].bitcast(I32), 0)
+        offs_sb = sb("offs_sb", [P, S // GROUP], U16)
+        nc.sync.dma_start(offs_sb[:], offs)
+        nc.sync.dma_start(scale_table[STAGE:STAGE_END, :].bitcast(I32), x_scales[0].bitcast(I32))
+        w3_raw = load_weight("w3", w3)
+        pos_sb = [load_list(i, pos) for i, pos in enumerate((pos1, pos2, pos3))]
+        word_table = sb("word_table", [P, T], I32)
+        nc.sync.dma_start(word_table[:], x_words[0].rearrange("p n t -> p (n t)").bitcast(I32))
+        w1_raw = load_weight("w1", w1)
+
+        x_scale = sb("x_scale", [P, S], U8)
+        nc.gpsimd.memset(x_scale[:].bitcast(I32), 0)
+        ident = sb("ident", [P, P], F32)
+        make_identity(nc, ident[:])
+        warm = sb("warm", [P, 1], F32)
+        nc.scalar.activation(warm[:], zero[:], ACT.Exp)
+
+        scale_picked = sb("scale_picked", [P, S], U8)
+        nc.vector.tensor_copy(scale_picked[:], scale_table[:].indirect(offs_sb[:]))
+        w3_grouped = interleave("w3", w3_raw, nc.vector.tensor_copy, "scale_table")
+        w3_mx = quantize("w3", w3_grouped)
+        w2_raw = load_weight("w2", w2, "w3_raw")
+        x_code = sb("x_code", [P, S], U32, "scale_table")
+        for j in range(ROWS):
+            nc.scalar.dma_start(
+                x_scale[j:P:QUADRANT, :].bitcast(I32), scale_picked[STAGE + j : STAGE_END : ROWS, :].bitcast(I32)
+            )
+        pt_sb = sb("pt_sb", [P, V], F32, "scale_picked")
+        nc.sync.dma_start(pt_sb[:], pt)
+
+        w1_grouped = interleave("w1", w1_raw, nc.scalar.copy)
+        a = sb("a", [P, S], F32, "w1_raw")
+        for h in range(2):
+            nc.vector.tensor_copy(x_code[:, half(h)], word_table[:].bitcast(U32).indirect(entries(offs_sb, half(h))))
+            for c in range(h * HALF // P, (h + 1) * HALF // P):
+                logits = bank("logits_at%d" % c, "logits%d" % c)
+                product(logits[:, :P], w3_mx, block(c))
+                nc.scalar.activation(a[:, block(c)], logits[:, :P], ACT.Exp, bias=zero[:])
+
+        w1_mx = quantize("w1", w1_grouped)
+        w2_grouped = interleave("w2", w2_raw, nc.vector.tensor_copy)
+        y_sb = sb("y_sb", [P, S], F32)
+        for h in range(2):
+            y = bank("y%d" % h, "y%d" % h)
+            product(y[:, :HALF], w1_mx, half(h))
+            nc.scalar.activation(y_sb[:, half(h)], y[:, :HALF], ACT.Copy)
+        w2_mx = quantize("w2", w2_grouped)
+        rr = sb("rr", [P, S], F32)
+        for h in range(2):
+            r = bank("r%d" % h, "r%d" % h)
+            product(r[:, :HALF], w2_mx, half(h))
+            nc.scalar.activation(rr[:, half(h)], r[:, :HALF], ACT.Relu)
+
+        a_at = [fetch("a_at", a, i) for i in range(LISTS)]
         den_t = [bank("den_t%d" % b, "logits%d" % b) for b in range(BLOCKS)]
         add_lists(den_t, a_at)
         root_t = [sb("root_t%d" % b, [P, P], F32) for b in range(BLOCKS)]
@@ -187,11 +198,10 @@ def tile_picked_box_p_kernel(
             add_transposed(pt_t[:, block(b)], [pt_sb[:, block(b)]])
         neg_pt_t = sb("neg_pt_t", [P, V], F32, "root_t0")
         nc.scalar.activation(neg_pt_t[:], pt_t[:, :V], ACT.Copy, scale=-1.0)
-
         neg_rr = sb("neg_rr", [P, S], F32, "root_t1")
         nc.scalar.activation(neg_rr[:], rr[:], ACT.Copy, scale=-1.0)
 
-        ya_at = [fetch_with("ya_at", y_sb, i, a_at[i], ALU.mult, BLOCKS if i == 2 else 1) for i in range(3)]
+        ya_at = [fetch_times("ya_at", y_sb, i, a_at[i], BLOCKS if i == LISTS - 1 else 1) for i in range(LISTS)]
         num_t = [bank("num_t%d" % b, "y%d" % b) for b in range(BLOCKS)]
         add_lists(num_t, ya_at)
 
@@ -205,14 +215,16 @@ def tile_picked_box_p_kernel(
             nc.vector.tensor_tensor(off01[:, block(b)], rr0[:, block(b)], rr1[:, block(b)], ALU.min)
 
         dist = sb("dist", [P, V], F32)
-        for b in range(BLOCKS):
-            dd = bank("dd%d" % b, ("logits2", "r1")[b])
+        for b, free_bank in enumerate(("logits2", "r1")):
+            dd = bank("dd%d" % b, free_bank)
             add_transposed(dd[:, :P], [neg_pt_t[:, block(b)], cen_t[b][:]])
             nc.scalar.activation(dist[:, block(b)], dd[:, :P], ACT.Abs)
+
         beyond2 = sb("beyond2", [P, V], F32)
         beyond01 = [sb("beyond01_%d" % b, [P, P], F32) for b in range(BLOCKS)]
-        for b, (cols, offsets) in enumerate(pieces_of(2, BLOCKS)):
-            nc.vector.tensor_tensor(beyond2[:, cols], neg_rr[:].indirect(offsets), dist[:, cols], ALU.add)
+        for b in range(BLOCKS):
+            offsets = entries(pos_sb[LISTS - 1], block(b))
+            nc.vector.tensor_tensor(beyond2[:, block(b)], neg_rr[:].indirect(offsets), dist[:, block(b)], ALU.add)
             nc.vector.tensor_tensor(beyond01[b][:], dist[:, block(b)], off01[:, block(b)], ALU.subtract)
         result = sb("result", [P, V], F32)
         for b in range(BLOCKS):

@@ -131,9 +131,9 @@ def tile_picked_box_p_kernel(
         scale_table = sb("scale_table", [P, T], U8)
         nc.gpsimd.memset(scale_table[0:STAGE, :].bitcast(I32), 0)
         nc.gpsimd.memset(scale_table[STAGE_END:P, :].bitcast(I32), 0)
+        nc.scalar.dma_start(scale_table[STAGE:STAGE_END, :].bitcast(I32), x_scales[0].bitcast(I32))
         offs_sb = sb("offs_sb", [P, S // GROUP], U16)
         nc.sync.dma_start(offs_sb[:], offs)
-        nc.sync.dma_start(scale_table[STAGE:STAGE_END, :].bitcast(I32), x_scales[0].bitcast(I32))
         w3_raw = load_weight("w3", w3)
         pos_sb = [load_list(i, pos) for i, pos in enumerate((pos1, pos2, pos3))]
         word_table = sb("word_table", [P, T], I32)

@@ -25,6 +25,7 @@ ROWS = 4
 BANK = 512
 LISTS = 3
 HALF = S // 2
+SPLIT = 80
 BLOCKS = V // P
 STAGE_END = P // 2
 STAGE = STAGE_END - K // QUADRANT
@@ -63,16 +64,22 @@ def tile_picked_box_p_kernel(
             nc.sync.dma_start(tile[:], pos)
             return tile
 
-        def interleave(name, raw, copy, tag=None):
+        def interleave(name, raw, shares, tag=None):
             grouped = sb(name + "_grouped", [P, N, PACK], BF16, tag)
-            copy(
-                grouped[:].rearrange("p (c i) j -> p c j i", i=RUN),
-                raw[:].rearrange("p j (c i) -> p c j i", i=RUN),
-            )
+            for copy, cols in shares:
+                copy(
+                    grouped[:, cols, :].rearrange("p (c i) j -> p c j i", i=RUN),
+                    raw[:, :, cols].rearrange("p j (c i) -> p c j i", i=RUN),
+                )
             return grouped
 
-        def quantize(name, grouped):
-            codes = sb(name + "_codes", [P, N], U32)
+        def gpsimd_copy(dst, src):
+            nc.gpsimd.tensor_scalar(dst, src, 1.0, 0.0, ALU.mult, ALU.add)
+
+        on_vector = [(nc.vector.tensor_copy, slice(0, N))]
+
+        def quantize(name, grouped, tag=None):
+            codes = sb(name + "_codes", [P, N], U32, tag)
             scales = sb(name + "_scales", [P, N], U8)
             nc.vector.quantize_mx(
                 out=codes[:].bitcast(FP8X4), scales=scales[:], in_=grouped[:].rearrange("p m j -> p (m j)")
@@ -135,10 +142,11 @@ def tile_picked_box_p_kernel(
         offs_sb = sb("offs_sb", [P, S // GROUP], U16)
         nc.sync.dma_start(offs_sb[:], offs)
         w3_raw = load_weight("w3", w3)
-        pos_sb = [load_list(i, pos) for i, pos in enumerate((pos1, pos2, pos3))]
+        pos_sb = [load_list(i, pos) for i, pos in enumerate((pos1, pos2))]
         word_table = sb("word_table", [P, T], I32)
         nc.sync.dma_start(word_table[:], x_words[0].rearrange("p n t -> p (n t)").bitcast(I32))
         w1_raw = load_weight("w1", w1)
+        pos_sb.append(load_list(LISTS - 1, pos3))
 
         x_scale = sb("x_scale", [P, S], U8)
         nc.gpsimd.memset(x_scale[:].bitcast(I32), 0)
@@ -149,7 +157,7 @@ def tile_picked_box_p_kernel(
 
         scale_picked = sb("scale_picked", [P, S], U8)
         nc.vector.tensor_copy(scale_picked[:], scale_table[:].indirect(offs_sb[:]))
-        w3_grouped = interleave("w3", w3_raw, nc.vector.tensor_copy, "scale_table")
+        w3_grouped = interleave("w3", w3_raw, on_vector, "scale_table")
         w3_mx = quantize("w3", w3_grouped)
         w2_raw = load_weight("w2", w2, "w3_raw")
         x_code = sb("x_code", [P, S], U32, "scale_table")
@@ -160,7 +168,7 @@ def tile_picked_box_p_kernel(
         pt_sb = sb("pt_sb", [P, V], F32, "scale_picked")
         nc.sync.dma_start(pt_sb[:], pt)
 
-        w1_grouped = interleave("w1", w1_raw, nc.scalar.copy)
+        w1_grouped = interleave("w1", w1_raw, [(nc.scalar.copy, slice(0, SPLIT)), (gpsimd_copy, slice(SPLIT, N))])
         a = sb("a", [P, S], F32, "w1_raw")
         for h in range(2):
             nc.vector.tensor_copy(x_code[:, half(h)], word_table[:].bitcast(U32).indirect(entries(offs_sb, half(h))))
@@ -170,35 +178,38 @@ def tile_picked_box_p_kernel(
                 nc.scalar.activation(a[:, block(c)], logits[:, :P], ACT.Exp, bias=zero[:])
 
         w1_mx = quantize("w1", w1_grouped)
-        w2_grouped = interleave("w2", w2_raw, nc.vector.tensor_copy)
+        w2_grouped = interleave("w2", w2_raw, on_vector)
         y_sb = sb("y_sb", [P, S], F32)
         for h in range(2):
             y = bank("y%d" % h, "y%d" % h)
             product(y[:, :HALF], w1_mx, half(h))
             nc.scalar.activation(y_sb[:, half(h)], y[:, :HALF], ACT.Copy)
-        w2_mx = quantize("w2", w2_grouped)
-        rr = sb("rr", [P, S], F32)
+        switch = sb("switch", [P, 1], F32, "w1_codes")
+        nc.scalar.activation(switch[:], a[:, S - 1 : S], ACT.Abs_reciprocal_sqrt)
+        w2_mx = quantize("w2", w2_grouped, "w1_grouped")
+        rr = sb("rr", [P, S], F32, "zero")
         for h in range(2):
             r = bank("r%d" % h, "r%d" % h)
             product(r[:, :HALF], w2_mx, half(h))
             nc.scalar.activation(rr[:, half(h)], r[:, :HALF], ACT.Relu)
 
-        a_at = [fetch("a_at", a, i) for i in range(LISTS)]
+        a_at = [fetch("a_at", a, i, "w3_raw" if i == 0 else None) for i in range(LISTS)]
         den_t = [bank("den_t%d" % b, "logits%d" % b) for b in range(BLOCKS)]
         add_lists(den_t, a_at)
-        root_t = [sb("root_t%d" % b, [P, P], F32) for b in range(BLOCKS)]
+        root_t = [sb("root_t%d" % b, [P, P], F32, tag) for b, tag in enumerate(("w1_grouped", "w2_scales"))]
         for b in range(BLOCKS):
             nc.scalar.activation(root_t[b][:], den_t[b][:, :P], ACT.Abs_reciprocal_sqrt)
+        pt_t = bank("pt_t", "logits3")
+        for b in range(BLOCKS):
+            add_transposed(pt_t[:, block(b)], [pt_sb[:, block(b)]])
+        neg_pt_t = [sb("neg_pt_t0", [P, P], F32, "x_scale")]
+        nc.scalar.activation(neg_pt_t[0][:], pt_t[:, block(0)], ACT.Copy, scale=-1.0)
         rec_t = [sb("rec_t%d" % b, [P, P], F32) for b in range(BLOCKS)]
         for b in range(BLOCKS):
             nc.scalar.activation(rec_t[b][:], root_t[b][:], ACT.Square)
-
-        pt_t = bank("pt_t", "r0")
-        for b in range(BLOCKS):
-            add_transposed(pt_t[:, block(b)], [pt_sb[:, block(b)]])
-        neg_pt_t = sb("neg_pt_t", [P, V], F32, "root_t0")
-        nc.scalar.activation(neg_pt_t[:], pt_t[:, :V], ACT.Copy, scale=-1.0)
-        neg_rr = sb("neg_rr", [P, S], F32, "root_t1")
+        neg_pt_t.append(sb("neg_pt_t1", [P, P], F32, "w1_grouped"))
+        nc.scalar.activation(neg_pt_t[1][:], pt_t[:, block(1)], ACT.Copy, scale=-1.0)
+        neg_rr = sb("neg_rr", [P, S], F32, "w2_scales")
         nc.scalar.activation(neg_rr[:], rr[:], ACT.Copy, scale=-1.0)
 
         ya_at = [fetch_times("ya_at", y_sb, i, a_at[i], BLOCKS if i == LISTS - 1 else 1) for i in range(LISTS)]
@@ -217,7 +228,7 @@ def tile_picked_box_p_kernel(
         dist = sb("dist", [P, V], F32)
         for b, free_bank in enumerate(("logits2", "r1")):
             dd = bank("dd%d" % b, free_bank)
-            add_transposed(dd[:, :P], [neg_pt_t[:, block(b)], cen_t[b][:]])
+            add_transposed(dd[:, :P], [neg_pt_t[b][:], cen_t[b][:]])
             nc.scalar.activation(dist[:, block(b)], dd[:, :P], ACT.Abs)
 
         beyond2 = sb("beyond2", [P, V], F32)

@@ -108,13 +108,10 @@ def tile_picked_box_p_kernel(
                 nc.vector.tensor_copy(picked[:, cols], table[:].indirect(entries(pos_sb[i], cols)))
             return picked
 
-        def fetch_times(name, table, i, factor, count):
-            picked = sb("%s%d" % (name, i), [P, V], F32)
-            for cols in pieces(count):
-                nc.vector.tensor_tensor(
-                    picked[:, cols], table[:].indirect(entries(pos_sb[i], cols)), factor[:, cols], ALU.mult
-                )
-            return picked
+        def fetch_times(picked, table, i, factor, cols):
+            nc.vector.tensor_tensor(
+                picked[:, cols], table[:].indirect(entries(pos_sb[i], cols)), factor[:, cols], ALU.mult
+            )
 
         def add_transposed(acc, terms):
             for i, term in enumerate(terms):
@@ -157,14 +154,14 @@ def tile_picked_box_p_kernel(
 
         scale_picked = sb("scale_picked", [P, S], U8)
         nc.vector.tensor_copy(scale_picked[:], scale_table[:].indirect(offs_sb[:]))
-        w3_grouped = interleave("w3", w3_raw, on_vector, "scale_table")
+        w3_grouped = interleave("w3", w3_raw, on_vector)
         w3_mx = quantize("w3", w3_grouped)
-        w2_raw = load_weight("w2", w2, "w3_raw")
-        x_code = sb("x_code", [P, S], U32, "scale_table")
+        x_code = sb("x_code", [P, S], U32, "w3_grouped")
         for j in range(ROWS):
-            nc.scalar.dma_start(
+            (nc.scalar, nc.sync)[j % 2].dma_start(
                 x_scale[j:P:QUADRANT, :].bitcast(I32), scale_picked[STAGE + j : STAGE_END : ROWS, :].bitcast(I32)
             )
+        w2_raw = load_weight("w2", w2, "scale_table")
         pt_sb = sb("pt_sb", [P, V], F32, "scale_picked")
         nc.sync.dma_start(pt_sb[:], pt)
 
@@ -193,7 +190,7 @@ def tile_picked_box_p_kernel(
             product(r[:, :HALF], w2_mx, half(h))
             nc.scalar.activation(rr[:, half(h)], r[:, :HALF], ACT.Relu)
 
-        a_at = [fetch("a_at", a, i, "w3_raw" if i == 0 else None) for i in range(LISTS)]
+        a_at = [fetch("a_at", a, i, "scale_table" if i == 0 else None) for i in range(LISTS)]
         den_t = [bank("den_t%d" % b, "logits%d" % b) for b in range(BLOCKS)]
         add_lists(den_t, a_at)
         root_t = [sb("root_t%d" % b, [P, P], F32, tag) for b, tag in enumerate(("w1_grouped", "w2_scales"))]
@@ -207,23 +204,29 @@ def tile_picked_box_p_kernel(
         rec_t = [sb("rec_t%d" % b, [P, P], F32) for b in range(BLOCKS)]
         for b in range(BLOCKS):
             nc.scalar.activation(rec_t[b][:], root_t[b][:], ACT.Square)
-        neg_pt_t.append(sb("neg_pt_t1", [P, P], F32, "w1_grouped"))
+        neg_pt_t.append(sb("neg_pt_t1", [P, P], F32, "w3_grouped"))
         nc.scalar.activation(neg_pt_t[1][:], pt_t[:, block(1)], ACT.Copy, scale=-1.0)
-        neg_rr = sb("neg_rr", [P, S], F32, "w2_scales")
+        neg_rr = sb("neg_rr", [P, S], F32)
         nc.scalar.activation(neg_rr[:], rr[:], ACT.Copy, scale=-1.0)
 
-        ya_at = [fetch_times("ya_at", y_sb, i, a_at[i], BLOCKS if i == LISTS - 1 else 1) for i in range(LISTS)]
+        ya_at = [sb("ya_at%d" % i, [P, V], F32) for i in range(LISTS)]
+        fetch_times(ya_at[0], y_sb, 0, a_at[0], slice(0, V))
+        for b in range(BLOCKS):
+            for i in range(1, LISTS):
+                fetch_times(ya_at[i], y_sb, i, a_at[i], block(b))
         num_t = [bank("num_t%d" % b, "y%d" % b) for b in range(BLOCKS)]
-        add_lists(num_t, ya_at)
+        for b in range(BLOCKS):
+            add_transposed(num_t[b][:, :P], [term[:, block(b)] for term in ya_at])
 
         rr0 = fetch("rr_at", rr, 0)
         cen_t = [sb("cen_t%d" % b, [P, P], F32) for b in range(BLOCKS)]
+        rr1 = [sb("rr_at1_%d" % b, [P, P], F32, tag) for b, tag in enumerate(("w1_grouped", "w2_scales"))]
         for b in range(BLOCKS):
             nc.vector.tensor_tensor(cen_t[b][:], num_t[b][:, :P], rec_t[b][:], ALU.mult)
-        rr1 = fetch("rr_at", rr, 1, "rec_t0", BLOCKS)
+            nc.vector.tensor_copy(rr1[b][:], rr[:].indirect(entries(pos_sb[1], block(b))))
         off01 = sb("off01", [P, V], F32)
         for b in range(BLOCKS):
-            nc.vector.tensor_tensor(off01[:, block(b)], rr0[:, block(b)], rr1[:, block(b)], ALU.min)
+            nc.vector.tensor_tensor(off01[:, block(b)], rr0[:, block(b)], rr1[b][:], ALU.min)
 
         dist = sb("dist", [P, V], F32)
         for b, free_bank in enumerate(("logits2", "r1")):
@@ -237,9 +240,9 @@ def tile_picked_box_p_kernel(
             offsets = entries(pos_sb[LISTS - 1], block(b))
             nc.vector.tensor_tensor(beyond2[:, block(b)], neg_rr[:].indirect(offsets), dist[:, block(b)], ALU.add)
             nc.vector.tensor_tensor(beyond01[b][:], dist[:, block(b)], off01[:, block(b)], ALU.subtract)
-        result = sb("result", [P, V], F32)
+        result = [sb("result%d" % b, [P, P], F32) for b in range(BLOCKS)]
         for b in range(BLOCKS):
             nc.vector.scalar_tensor_tensor(
-                result[:, block(b)], beyond2[:, block(b)], 0.0, beyond01[b][:], ALU.max, ALU.max
+                result[b][:], beyond2[:, block(b)], 0.0, beyond01[b][:], ALU.max, ALU.max
             )
-        nc.sync.dma_start(out, result[:])
+            (nc.scalar, nc.sync)[b].dma_start(out[:, block(b)], result[b][:])

@@ -154,14 +154,14 @@ def tile_picked_box_p_kernel(
 
         scale_picked = sb("scale_picked", [P, S], U8)
         nc.vector.tensor_copy(scale_picked[:], scale_table[:].indirect(offs_sb[:]))
-        w3_grouped = interleave("w3", w3_raw, on_vector)
+        w3_grouped = interleave("w3", w3_raw, on_vector, "scale_table")
         w3_mx = quantize("w3", w3_grouped)
-        x_code = sb("x_code", [P, S], U32, "w3_grouped")
+        w2_raw = load_weight("w2", w2, "w3_raw")
+        x_code = sb("x_code", [P, S], U32, "scale_table")
         for j in range(ROWS):
-            (nc.scalar, nc.sync)[j % 2].dma_start(
+            nc.scalar.dma_start(
                 x_scale[j:P:QUADRANT, :].bitcast(I32), scale_picked[STAGE + j : STAGE_END : ROWS, :].bitcast(I32)
             )
-        w2_raw = load_weight("w2", w2, "scale_table")
         pt_sb = sb("pt_sb", [P, V], F32, "scale_picked")
         nc.sync.dma_start(pt_sb[:], pt)
 
@@ -190,7 +190,7 @@ def tile_picked_box_p_kernel(
             product(r[:, :HALF], w2_mx, half(h))
             nc.scalar.activation(rr[:, half(h)], r[:, :HALF], ACT.Relu)
 
-        a_at = [fetch("a_at", a, i, "scale_table" if i == 0 else None) for i in range(LISTS)]
+        a_at = [fetch("a_at", a, i, "w3_raw" if i == 0 else None) for i in range(LISTS)]
         den_t = [bank("den_t%d" % b, "logits%d" % b) for b in range(BLOCKS)]
         add_lists(den_t, a_at)
         root_t = [sb("root_t%d" % b, [P, P], F32, tag) for b, tag in enumerate(("w1_grouped", "w2_scales"))]
@@ -204,7 +204,7 @@ def tile_picked_box_p_kernel(
         rec_t = [sb("rec_t%d" % b, [P, P], F32) for b in range(BLOCKS)]
         for b in range(BLOCKS):
             nc.scalar.activation(rec_t[b][:], root_t[b][:], ACT.Square)
-        neg_pt_t.append(sb("neg_pt_t1", [P, P], F32, "w3_grouped"))
+        neg_pt_t.append(sb("neg_pt_t1", [P, P], F32, "scale_table"))
         nc.scalar.activation(neg_pt_t[1][:], pt_t[:, block(1)], ACT.Copy, scale=-1.0)
         neg_rr = sb("neg_rr", [P, S], F32)
         nc.scalar.activation(neg_rr[:], rr[:], ACT.Copy, scale=-1.0)
@@ -240,9 +240,9 @@ def tile_picked_box_p_kernel(
             offsets = entries(pos_sb[LISTS - 1], block(b))
             nc.vector.tensor_tensor(beyond2[:, block(b)], neg_rr[:].indirect(offsets), dist[:, block(b)], ALU.add)
             nc.vector.tensor_tensor(beyond01[b][:], dist[:, block(b)], off01[:, block(b)], ALU.subtract)
-        result = [sb("result%d" % b, [P, P], F32) for b in range(BLOCKS)]
+        result = sb("result", [P, V], F32)
         for b in range(BLOCKS):
             nc.vector.scalar_tensor_tensor(
-                result[b][:], beyond2[:, block(b)], 0.0, beyond01[b][:], ALU.max, ALU.max
+                result[:, block(b)], beyond2[:, block(b)], 0.0, beyond01[b][:], ALU.max, ALU.max
             )
-            (nc.scalar, nc.sync)[b].dma_start(out[:, block(b)], result[b][:])
+        nc.sync.dma_start(out, result[:])

@@ -147,6 +147,8 @@ def tile_picked_box_p_kernel(
 
         x_scale = sb("x_scale", [P, S], U8)
         nc.gpsimd.memset(x_scale[:].bitcast(I32), 0)
+        abs_bias = sb("abs_bias", [P, 1], F32)
+        nc.gpsimd.memset(abs_bias[:], 0.0)
         ident = sb("ident", [P, P], F32)
         make_identity(nc, ident[:])
         warm = sb("warm", [P, 1], F32)
@@ -218,28 +220,30 @@ def tile_picked_box_p_kernel(
         for b in range(BLOCKS):
             add_transposed(num_t[b][:, :P], [term[:, block(b)] for term in ya_at])
 
-        rr0 = fetch("rr_at", rr, 0)
+        rr0 = [sb("rr_at0_%d" % b, [P, P], F32, tag) for b, tag in enumerate((None, "w1_grouped"))]
         cen_t = [sb("cen_t%d" % b, [P, P], F32) for b in range(BLOCKS)]
-        rr1 = [sb("rr_at1_%d" % b, [P, P], F32, tag) for b, tag in enumerate(("w1_grouped", "w2_scales"))]
         for b in range(BLOCKS):
+            nc.vector.tensor_copy(rr0[b][:], rr[:].indirect(entries(pos_sb[0], block(b))))
             nc.vector.tensor_tensor(cen_t[b][:], num_t[b][:, :P], rec_t[b][:], ALU.mult)
-            nc.vector.tensor_copy(rr1[b][:], rr[:].indirect(entries(pos_sb[1], block(b))))
-        off01 = sb("off01", [P, V], F32)
-        for b in range(BLOCKS):
-            nc.vector.tensor_tensor(off01[:, block(b)], rr0[:, block(b)], rr1[b][:], ALU.min)
+        rr1 = fetch("rr_at", rr, 1, "w2_scales", BLOCKS)
 
         dist = sb("dist", [P, V], F32)
         for b, free_bank in enumerate(("logits2", "r1")):
             dd = bank("dd%d" % b, free_bank)
             add_transposed(dd[:, :P], [neg_pt_t[b][:], cen_t[b][:]])
-            nc.scalar.activation(dist[:, block(b)], dd[:, :P], ACT.Abs)
+            nc.scalar.activation(dist[:, block(b)], dd[:, :P], ACT.Abs, bias=abs_bias[:] if b == 0 else 0.0)
 
         beyond2 = sb("beyond2", [P, V], F32)
+        off01 = [sb("off01_%d" % b, [P, P], F32, tag) for b, tag in enumerate((None, "abs_bias"))]
         beyond01 = [sb("beyond01_%d" % b, [P, P], F32) for b in range(BLOCKS)]
         for b in range(BLOCKS):
             offsets = entries(pos_sb[LISTS - 1], block(b))
+            if b == 0:
+                nc.vector.tensor_tensor(off01[0][:], rr0[0][:], rr1[:, block(0)], ALU.min)
             nc.vector.tensor_tensor(beyond2[:, block(b)], neg_rr[:].indirect(offsets), dist[:, block(b)], ALU.add)
-            nc.vector.tensor_tensor(beyond01[b][:], dist[:, block(b)], off01[:, block(b)], ALU.subtract)
+            if b == 0:
+                nc.vector.tensor_tensor(off01[1][:], rr0[1][:], rr1[:, block(1)], ALU.min)
+            nc.vector.tensor_tensor(beyond01[b][:], dist[:, block(b)], off01[b][:], ALU.subtract)
         result = sb("result", [P, V], F32)
         for b in range(BLOCKS):
             nc.vector.scalar_tensor_tensor(

@@ -149,6 +149,8 @@ def tile_picked_box_p_kernel(
         nc.gpsimd.memset(x_scale[:].bitcast(I32), 0)
         abs_bias = sb("abs_bias", [P, 1], F32)
         nc.gpsimd.memset(abs_bias[:], 0.0)
+        square_bias = sb("square_bias", [P, 1], F32)
+        nc.gpsimd.memset(square_bias[:], 0.0)
         ident = sb("ident", [P, P], F32)
         make_identity(nc, ident[:])
         warm = sb("warm", [P, 1], F32)
@@ -183,8 +185,6 @@ def tile_picked_box_p_kernel(
             y = bank("y%d" % h, "y%d" % h)
             product(y[:, :HALF], w1_mx, half(h))
             nc.scalar.activation(y_sb[:, half(h)], y[:, :HALF], ACT.Copy)
-        switch = sb("switch", [P, 1], F32, "w1_codes")
-        nc.scalar.activation(switch[:], a[:, S - 1 : S], ACT.Abs_reciprocal_sqrt)
         w2_mx = quantize("w2", w2_grouped, "w1_grouped")
         rr = sb("rr", [P, S], F32, "zero")
         for h in range(2):
@@ -205,10 +205,10 @@ def tile_picked_box_p_kernel(
         nc.scalar.activation(neg_pt_t[0][:], pt_t[:, block(0)], ACT.Copy, scale=-1.0)
         rec_t = [sb("rec_t%d" % b, [P, P], F32) for b in range(BLOCKS)]
         for b in range(BLOCKS):
-            nc.scalar.activation(rec_t[b][:], root_t[b][:], ACT.Square)
+            nc.scalar.activation(rec_t[b][:], root_t[b][:], ACT.Square, bias=square_bias[:])
         neg_pt_t.append(sb("neg_pt_t1", [P, P], F32, "scale_table"))
         nc.scalar.activation(neg_pt_t[1][:], pt_t[:, block(1)], ACT.Copy, scale=-1.0)
-        neg_rr = sb("neg_rr", [P, S], F32)
+        neg_rr = sb("neg_rr", [P, S], F32, "square_bias")
         nc.scalar.activation(neg_rr[:], rr[:], ACT.Copy, scale=-1.0)
 
         ya_at = [sb("ya_at%d" % i, [P, V], F32) for i in range(LISTS)]

@@ -1,7 +1,6 @@
 from contextlib import ExitStack
 
 import concourse.mybir as mybir
-from concourse.masks import make_identity
 
 K, T, S, V, N = 512, 2048, 512, 256, 128
 FLOPS = 3 * 2 * K * N * S
@@ -26,7 +25,8 @@ BANK = 512
 LISTS = 3
 HALF = S // 2
 SPLIT = 80
-BLOCKS = V // P
+BLOCKS = 2
+WIDTH = V // BLOCKS
 STAGE_END = P // 2
 STAGE = STAGE_END - K // QUADRANT
 
@@ -42,11 +42,11 @@ def tile_picked_box_p_kernel(
         def sb(name, shape, dtype, tag=None):
             return keep.tile(shape, dtype, name=name, tag=tag or name, align_bytes=64)
 
-        def bank(name, tag):
-            return psum.tile([P, BANK], F32, name=name, tag=tag)
+        def bank(name):
+            return psum.tile([P, BANK], F32, name=name, tag=name)
 
         def block(b):
-            return slice(b * P, (b + 1) * P)
+            return slice(b * WIDTH, (b + 1) * WIDTH)
 
         def half(h):
             return slice(h * HALF, (h + 1) * HALF)
@@ -98,39 +98,24 @@ def tile_picked_box_p_kernel(
                 stop=True,
             )
 
-        def pieces(count):
-            width = V // count
-            return [slice(c * width, (c + 1) * width) for c in range(count)]
+        def blocks(name, tags=(None, None)):
+            return [sb("%s%d" % (name, b), [P, WIDTH], F32, tags[b]) for b in range(BLOCKS)]
 
-        def fetch(name, table, i, tag=None, count=1):
-            picked = sb("%s%d" % (name, i), [P, V], F32, tag)
-            for cols in pieces(count):
-                nc.vector.tensor_copy(picked[:, cols], table[:].indirect(entries(pos_sb[i], cols)))
-            return picked
+        def at(table, i, cols):
+            return table[:].indirect(entries(pos_sb[i], cols))
 
-        def fetch_times(picked, table, i, factor, cols):
-            nc.vector.tensor_tensor(
-                picked[:, cols], table[:].indirect(entries(pos_sb[i], cols)), factor[:, cols], ALU.mult
-            )
+        def fetch_add(name, table, i, partial, tags=(None, None)):
+            total = blocks(name, tags)
+            for b in range(BLOCKS):
+                nc.vector.tensor_tensor(total[b][:], at(table, i, block(b)), partial[b], ALU.add)
+            return [t[:] for t in total]
 
-        def add_transposed(acc, terms):
-            for i, term in enumerate(terms):
-                nc.tensor.matmul(acc, term, ident[:], is_transpose=True, start=(i == 0), stop=(i == len(terms) - 1))
+        def zero_column(name):
+            column = sb(name, [P, 1], F32)
+            nc.gpsimd.memset(column[:], 0.0)
+            return column
 
-        def add_lists(banks, picked):
-            for i, term in enumerate(picked):
-                for b in range(BLOCKS):
-                    nc.tensor.matmul(
-                        banks[b][:, :P],
-                        term[:, block(b)],
-                        ident[:],
-                        is_transpose=True,
-                        start=(i == 0),
-                        stop=(i == LISTS - 1),
-                    )
-
-        zero = sb("zero", [P, 1], F32)
-        nc.gpsimd.memset(zero[:], 0.0)
+        zero = zero_column("zero")
 
         scale_table = sb("scale_table", [P, T], U8)
         nc.gpsimd.memset(scale_table[0:STAGE, :].bitcast(I32), 0)
@@ -147,12 +132,7 @@ def tile_picked_box_p_kernel(
 
         x_scale = sb("x_scale", [P, S], U8)
         nc.gpsimd.memset(x_scale[:].bitcast(I32), 0)
-        abs_bias = sb("abs_bias", [P, 1], F32)
-        nc.gpsimd.memset(abs_bias[:], 0.0)
-        square_bias = sb("square_bias", [P, 1], F32)
-        nc.gpsimd.memset(square_bias[:], 0.0)
-        ident = sb("ident", [P, P], F32)
-        make_identity(nc, ident[:])
+        square_bias = zero_column("square_bias")
         warm = sb("warm", [P, 1], F32)
         nc.scalar.activation(warm[:], zero[:], ACT.Exp)
 
@@ -174,79 +154,69 @@ def tile_picked_box_p_kernel(
         for h in range(2):
             nc.vector.tensor_copy(x_code[:, half(h)], word_table[:].bitcast(U32).indirect(entries(offs_sb, half(h))))
             for c in range(h * HALF // P, (h + 1) * HALF // P):
-                logits = bank("logits_at%d" % c, "logits%d" % c)
-                product(logits[:, :P], w3_mx, block(c))
-                nc.scalar.activation(a[:, block(c)], logits[:, :P], ACT.Exp, bias=zero[:])
+                cols = slice(c * P, (c + 1) * P)
+                logits = bank("logits%d" % c)
+                product(logits[:, :P], w3_mx, cols)
+                nc.scalar.activation(a[:, cols], logits[:, :P], ACT.Exp, bias=zero[:])
 
         w1_mx = quantize("w1", w1_grouped)
         w2_grouped = interleave("w2", w2_raw, on_vector)
-        y_sb = sb("y_sb", [P, S], F32)
+        y = [bank("y%d" % h) for h in range(2)]
         for h in range(2):
-            y = bank("y%d" % h, "y%d" % h)
-            product(y[:, :HALF], w1_mx, half(h))
-            nc.scalar.activation(y_sb[:, half(h)], y[:, :HALF], ACT.Copy)
+            product(y[h][:, :HALF], w1_mx, half(h))
         w2_mx = quantize("w2", w2_grouped, "w1_grouped")
+        r = bank("r")
+        product(r[:], w2_mx, slice(0, S))
+        every = slice(0, V)
+
+        ya = sb("ya", [P, S], F32, "w2_grouped")
+        a0 = sb("a0", [P, V], F32)
+        nc.scalar.activation(a0[:], at(a, 0, every), ACT.Copy)
         rr = sb("rr", [P, S], F32, "zero")
+        nc.scalar.activation(rr[:], r[:], ACT.Relu)
         for h in range(2):
-            r = bank("r%d" % h, "r%d" % h)
-            product(r[:, :HALF], w2_mx, half(h))
-            nc.scalar.activation(rr[:, half(h)], r[:, :HALF], ACT.Relu)
+            nc.vector.tensor_tensor(ya[:, half(h)], y[h][:, :HALF], a[:, half(h)], ALU.mult)
+        ya0 = sb("ya0", [P, V], F32)
+        nc.vector.tensor_copy(ya0[:], at(ya, 0, every))
+        a01 = fetch_add("a01_", a, 1, [a0[:, block(b)] for b in range(BLOCKS)])
+        den = fetch_add("den", a, 2, a01)
+        root = blocks("root", ("w1_grouped", "w2_scales"))
+        for b in range(BLOCKS):
+            nc.scalar.activation(root[b][:], den[b], ACT.Abs_reciprocal_sqrt)
+        rec = blocks("rec", ("den0", "den1"))
+        nc.scalar.activation(rec[0][:], root[0][:], ACT.Square, bias=square_bias[:])
+        nc.scalar.activation(rec[1][:], root[1][:], ACT.Square)
 
-        a_at = [fetch("a_at", a, i, "w3_raw" if i == 0 else None) for i in range(LISTS)]
-        den_t = [bank("den_t%d" % b, "logits%d" % b) for b in range(BLOCKS)]
-        add_lists(den_t, a_at)
-        root_t = [sb("root_t%d" % b, [P, P], F32, tag) for b, tag in enumerate(("w1_grouped", "w2_scales"))]
-        for b in range(BLOCKS):
-            nc.scalar.activation(root_t[b][:], den_t[b][:, :P], ACT.Abs_reciprocal_sqrt)
-        pt_t = bank("pt_t", "logits3")
-        for b in range(BLOCKS):
-            add_transposed(pt_t[:, block(b)], [pt_sb[:, block(b)]])
-        neg_pt_t = [sb("neg_pt_t0", [P, P], F32, "x_scale")]
-        nc.scalar.activation(neg_pt_t[0][:], pt_t[:, block(0)], ACT.Copy, scale=-1.0)
-        rec_t = [sb("rec_t%d" % b, [P, P], F32) for b in range(BLOCKS)]
-        for b in range(BLOCKS):
-            nc.scalar.activation(rec_t[b][:], root_t[b][:], ACT.Square, bias=square_bias[:])
-        neg_pt_t.append(sb("neg_pt_t1", [P, P], F32, "scale_table"))
-        nc.scalar.activation(neg_pt_t[1][:], pt_t[:, block(1)], ACT.Copy, scale=-1.0)
-        neg_rr = sb("neg_rr", [P, S], F32, "square_bias")
-        nc.scalar.activation(neg_rr[:], rr[:], ACT.Copy, scale=-1.0)
+        ya01 = fetch_add("ya01_", ya, 1, [ya0[:, block(b)] for b in range(BLOCKS)], ("a0", "a01_0"))
+        num = fetch_add("num", ya, 2, ya01)
 
-        ya_at = [sb("ya_at%d" % i, [P, V], F32) for i in range(LISTS)]
-        fetch_times(ya_at[0], y_sb, 0, a_at[0], slice(0, V))
-        for b in range(BLOCKS):
-            for i in range(1, LISTS):
-                fetch_times(ya_at[i], y_sb, i, a_at[i], block(b))
-        num_t = [bank("num_t%d" % b, "y%d" % b) for b in range(BLOCKS)]
-        for b in range(BLOCKS):
-            add_transposed(num_t[b][:, :P], [term[:, block(b)] for term in ya_at])
+        rr01 = sb("rr01", [P, 2 * V], F32, "square_bias")
+        rr0, rr1 = rr01[:, :V], rr01[:, V:]
+        nc.scalar.activation(rr0, at(rr, 0, every), ACT.Copy)
+        nc.scalar.activation(rr1, at(rr, 1, every), ACT.Copy)
 
-        rr0 = [sb("rr_at0_%d" % b, [P, P], F32, tag) for b, tag in enumerate((None, "w1_grouped"))]
-        cen_t = [sb("cen_t%d" % b, [P, P], F32) for b in range(BLOCKS)]
+        cen = blocks("cen")
+        rr2 = blocks("rr2_", ("w1_grouped", "w2_scales"))
+        dd = blocks("dd")
         for b in range(BLOCKS):
-            nc.vector.tensor_copy(rr0[b][:], rr[:].indirect(entries(pos_sb[0], block(b))))
-            nc.vector.tensor_tensor(cen_t[b][:], num_t[b][:, :P], rec_t[b][:], ALU.mult)
-        rr1 = fetch("rr_at", rr, 1, "w2_scales", BLOCKS)
-
-        dist = sb("dist", [P, V], F32)
-        for b, free_bank in enumerate(("logits2", "r1")):
-            dd = bank("dd%d" % b, free_bank)
-            add_transposed(dd[:, :P], [neg_pt_t[b][:], cen_t[b][:]])
-            nc.scalar.activation(dist[:, block(b)], dd[:, :P], ACT.Abs, bias=abs_bias[:] if b == 0 else 0.0)
-
-        beyond2 = sb("beyond2", [P, V], F32)
-        off01 = [sb("off01_%d" % b, [P, P], F32, tag) for b, tag in enumerate((None, "abs_bias"))]
-        beyond01 = [sb("beyond01_%d" % b, [P, P], F32) for b in range(BLOCKS)]
+            nc.vector.tensor_tensor(cen[b][:], num[b], rec[b][:], ALU.mult)
+            nc.vector.tensor_copy(rr2[b][:], at(rr, 2, block(b)))
+            nc.gpsimd.tensor_tensor(dd[b][:], cen[b][:], pt_sb[:, block(b)], ALU.subtract)
+        dist = blocks("dist")
         for b in range(BLOCKS):
-            offsets = entries(pos_sb[LISTS - 1], block(b))
-            if b == 0:
-                nc.vector.tensor_tensor(off01[0][:], rr0[0][:], rr1[:, block(0)], ALU.min)
-            nc.vector.tensor_tensor(beyond2[:, block(b)], neg_rr[:].indirect(offsets), dist[:, block(b)], ALU.add)
-            if b == 0:
-                nc.vector.tensor_tensor(off01[1][:], rr0[1][:], rr1[:, block(1)], ALU.min)
-            nc.vector.tensor_tensor(beyond01[b][:], dist[:, block(b)], off01[b][:], ALU.subtract)
+            nc.scalar.activation(dist[b][:], dd[b][:], ACT.Abs)
+
+        off02 = blocks("off02_")
+        for b in range(BLOCKS):
+            nc.vector.tensor_tensor(off02[b][:], rr0[:, block(b)], rr2[b][:], ALU.min)
+        beyond1 = blocks("beyond1_")
+        beyond02 = blocks("beyond02_")
+        for b in range(BLOCKS):
+            nc.vector.tensor_tensor(beyond1[b][:], dist[b][:], rr1[:, block(b)], ALU.subtract)
+            nc.vector.tensor_tensor(beyond02[b][:], dist[b][:], off02[b][:], ALU.subtract)
         result = sb("result", [P, V], F32)
         for b in range(BLOCKS):
             nc.vector.scalar_tensor_tensor(
-                result[:, block(b)], beyond2[:, block(b)], 0.0, beyond01[b][:], ALU.max, ALU.max
+                result[:, block(b)], beyond1[b][:], 0.0, beyond02[b][:], ALU.max, ALU.max
             )
         nc.sync.dma_start(out, result[:])

@@ -104,11 +104,11 @@ def tile_picked_box_p_kernel(
         def at(table, i, cols):
             return table[:].indirect(entries(pos_sb[i], cols))
 
-        def fetch_add(name, table, i, partial, tags=(None, None)):
+        def fetch_with(name, table, i, partial, op, tags=(None, None)):
             total = blocks(name, tags)
             for b in range(BLOCKS):
-                nc.vector.tensor_tensor(total[b][:], at(table, i, block(b)), partial[b], ALU.add)
-            return [t[:] for t in total]
+                nc.vector.tensor_tensor(total[b][:], at(table, i, block(b)), partial[b][:], op)
+            return total
 
         def zero_column(name):
             column = sb(name, [P, 1], F32)
@@ -127,12 +127,11 @@ def tile_picked_box_p_kernel(
         pos_sb = [load_list(i, pos) for i, pos in enumerate((pos1, pos2))]
         word_table = sb("word_table", [P, T], I32)
         nc.sync.dma_start(word_table[:], x_words[0].rearrange("p n t -> p (n t)").bitcast(I32))
-        w1_raw = load_weight("w1", w1)
+        w2_raw = load_weight("w2", w2)
         pos_sb.append(load_list(LISTS - 1, pos3))
 
         x_scale = sb("x_scale", [P, S], U8)
         nc.gpsimd.memset(x_scale[:].bitcast(I32), 0)
-        square_bias = zero_column("square_bias")
         warm = sb("warm", [P, 1], F32)
         nc.scalar.activation(warm[:], zero[:], ACT.Exp)
 
@@ -140,7 +139,7 @@ def tile_picked_box_p_kernel(
         nc.vector.tensor_copy(scale_picked[:], scale_table[:].indirect(offs_sb[:]))
         w3_grouped = interleave("w3", w3_raw, on_vector, "scale_table")
         w3_mx = quantize("w3", w3_grouped)
-        w2_raw = load_weight("w2", w2, "w3_raw")
+        w1_raw = load_weight("w1", w1, "w3_raw")
         x_code = sb("x_code", [P, S], U32, "scale_table")
         for j in range(ROWS):
             nc.scalar.dma_start(
@@ -149,8 +148,8 @@ def tile_picked_box_p_kernel(
         pt_sb = sb("pt_sb", [P, V], F32, "scale_picked")
         nc.sync.dma_start(pt_sb[:], pt)
 
-        w1_grouped = interleave("w1", w1_raw, [(nc.scalar.copy, slice(0, SPLIT)), (gpsimd_copy, slice(SPLIT, N))])
-        a = sb("a", [P, S], F32, "w1_raw")
+        w2_grouped = interleave("w2", w2_raw, [(nc.scalar.copy, slice(0, SPLIT)), (gpsimd_copy, slice(SPLIT, N))])
+        a = sb("a", [P, S], F32, "w2_raw")
         for h in range(2):
             nc.vector.tensor_copy(x_code[:, half(h)], word_table[:].bitcast(U32).indirect(entries(offs_sb, half(h))))
             for c in range(h * HALF // P, (h + 1) * HALF // P):
@@ -159,64 +158,61 @@ def tile_picked_box_p_kernel(
                 product(logits[:, :P], w3_mx, cols)
                 nc.scalar.activation(a[:, cols], logits[:, :P], ACT.Exp, bias=zero[:])
 
-        w1_mx = quantize("w1", w1_grouped)
-        w2_grouped = interleave("w2", w2_raw, on_vector)
+        w2_mx = quantize("w2", w2_grouped)
+        w1_grouped = interleave("w1", w1_raw, on_vector)
+        r = [bank("r%d" % h) for h in range(2)]
+        for h in range(2):
+            product(r[h][:, :HALF], w2_mx, half(h))
+        w1_mx = quantize("w1", w1_grouped, "w2_grouped")
         y = [bank("y%d" % h) for h in range(2)]
         for h in range(2):
             product(y[h][:, :HALF], w1_mx, half(h))
-        w2_mx = quantize("w2", w2_grouped, "w1_grouped")
-        r = bank("r")
-        product(r[:], w2_mx, slice(0, S))
         every = slice(0, V)
 
-        ya = sb("ya", [P, S], F32, "w2_grouped")
-        a0 = sb("a0", [P, V], F32)
-        nc.scalar.activation(a0[:], at(a, 0, every), ACT.Copy)
         rr = sb("rr", [P, S], F32, "zero")
-        nc.scalar.activation(rr[:], r[:], ACT.Relu)
+        for h in range(2):
+            nc.scalar.activation(rr[:, half(h)], r[h][:, :HALF], ACT.Relu)
+        rr_at = [sb("rr_at%d" % i, [P, V], F32) for i in range(LISTS)]
+        for i in range(LISTS):
+            nc.scalar.activation(rr_at[i][:], at(rr, i, every), ACT.Copy)
+
+        a0 = blocks("a0_", ("w3_raw", None))
+        for b in range(BLOCKS):
+            nc.vector.tensor_copy(a0[b][:], at(a, 0, block(b)))
+        a01 = fetch_with("a01_", a, 1, a0, ALU.add)
+        den = fetch_with("den", a, 2, a01, ALU.add)
+        ya = sb("ya", [P, S], F32, "a01_0")
         for h in range(2):
             nc.vector.tensor_tensor(ya[:, half(h)], y[h][:, :HALF], a[:, half(h)], ALU.mult)
-        ya0 = sb("ya0", [P, V], F32)
-        nc.vector.tensor_copy(ya0[:], at(ya, 0, every))
-        a01 = fetch_add("a01_", a, 1, [a0[:, block(b)] for b in range(BLOCKS)])
-        den = fetch_add("den", a, 2, a01)
-        root = blocks("root", ("w1_grouped", "w2_scales"))
+        pt_den = blocks("pt_den")
         for b in range(BLOCKS):
-            nc.scalar.activation(root[b][:], den[b], ACT.Abs_reciprocal_sqrt)
-        rec = blocks("rec", ("den0", "den1"))
-        nc.scalar.activation(rec[0][:], root[0][:], ACT.Square, bias=square_bias[:])
-        nc.scalar.activation(rec[1][:], root[1][:], ACT.Square)
+            nc.gpsimd.tensor_tensor(pt_den[b][:], pt_sb[:, block(b)], den[b][:], ALU.mult)
 
-        ya01 = fetch_add("ya01_", ya, 1, [ya0[:, block(b)] for b in range(BLOCKS)], ("a0", "a01_0"))
-        num = fetch_add("num", ya, 2, ya01)
+        root = sb("root", [P, V], F32, "zero")
+        for b in range(BLOCKS):
+            nc.scalar.activation(root[:, block(b)], den[b][:], ACT.Abs_reciprocal_sqrt)
+        rec = blocks("rec")
+        for b in range(BLOCKS):
+            nc.scalar.activation(rec[b][:], root[:, block(b)], ACT.Square)
 
-        rr01 = sb("rr01", [P, 2 * V], F32, "square_bias")
-        rr0, rr1 = rr01[:, :V], rr01[:, V:]
-        nc.scalar.activation(rr0, at(rr, 0, every), ACT.Copy)
-        nc.scalar.activation(rr1, at(rr, 1, every), ACT.Copy)
+        off01 = sb("off01", [P, V], F32, "a01_1")
+        nc.vector.tensor_tensor(off01[:], rr_at[0][:], rr_at[1][:], ALU.min)
+        gap0 = fetch_with("gap0_", ya, 0, pt_den, ALU.subtract)
+        off = sb("off", [P, V], F32, "pt_den0")
+        nc.vector.tensor_tensor(off[:], off01[:], rr_at[2][:], ALU.min)
+        gap01 = fetch_with("gap01_", ya, 1, gap0, ALU.add)
+        gap = fetch_with("gap", ya, 2, gap01, ALU.add)
+        size = blocks("size")
+        for b in range(BLOCKS):
+            nc.scalar.activation(size[b][:], gap[b][:], ACT.Abs)
 
-        cen = blocks("cen")
-        rr2 = blocks("rr2_", ("w1_grouped", "w2_scales"))
-        dd = blocks("dd")
+        off_den = sb("off_den", [P, V], F32, "gap01_0")
         for b in range(BLOCKS):
-            nc.vector.tensor_tensor(cen[b][:], num[b], rec[b][:], ALU.mult)
-            nc.vector.tensor_copy(rr2[b][:], at(rr, 2, block(b)))
-            nc.gpsimd.tensor_tensor(dd[b][:], cen[b][:], pt_sb[:, block(b)], ALU.subtract)
-        dist = blocks("dist")
+            nc.vector.tensor_tensor(off_den[:, block(b)], off[:, block(b)], den[b][:], ALU.mult)
+        beyond = blocks("beyond")
         for b in range(BLOCKS):
-            nc.scalar.activation(dist[b][:], dd[b][:], ACT.Abs)
-
-        off02 = blocks("off02_")
+            nc.vector.tensor_tensor(beyond[b][:], size[b][:], off_den[:, block(b)], ALU.subtract)
+        result = sb("result", [P, V], F32, "gap1")
         for b in range(BLOCKS):
-            nc.vector.tensor_tensor(off02[b][:], rr0[:, block(b)], rr2[b][:], ALU.min)
-        beyond1 = blocks("beyond1_")
-        beyond02 = blocks("beyond02_")
-        for b in range(BLOCKS):
-            nc.vector.tensor_tensor(beyond1[b][:], dist[b][:], rr1[:, block(b)], ALU.subtract)
-            nc.vector.tensor_tensor(beyond02[b][:], dist[b][:], off02[b][:], ALU.subtract)
-        result = sb("result", [P, V], F32)
-        for b in range(BLOCKS):
-            nc.vector.scalar_tensor_tensor(
-                result[:, block(b)], beyond1[b][:], 0.0, beyond02[b][:], ALU.max, ALU.max
-            )
+            nc.vector.scalar_tensor_tensor(result[:, block(b)], beyond[b][:], 0.0, rec[b][:], ALU.max, ALU.mult)
         nc.sync.dma_start(out, result[:])

@@ -24,7 +24,6 @@ ROWS = 4
 BANK = 512
 LISTS = 3
 HALF = S // 2
-SPLIT = 80
 BLOCKS = 2
 WIDTH = V // BLOCKS
 STAGE_END = P // 2
@@ -72,9 +71,6 @@ def tile_picked_box_p_kernel(
                     raw[:, :, cols].rearrange("p j (c i) -> p c j i", i=RUN),
                 )
             return grouped
-
-        def gpsimd_copy(dst, src):
-            nc.gpsimd.tensor_scalar(dst, src, 1.0, 0.0, ALU.mult, ALU.add)
 
         on_vector = [(nc.vector.tensor_copy, slice(0, N))]
 
@@ -148,7 +144,7 @@ def tile_picked_box_p_kernel(
         pt_sb = sb("pt_sb", [P, V], F32, "scale_picked")
         nc.sync.dma_start(pt_sb[:], pt)
 
-        w2_grouped = interleave("w2", w2_raw, [(nc.scalar.copy, slice(0, SPLIT)), (gpsimd_copy, slice(SPLIT, N))])
+        w2_grouped = interleave("w2", w2_raw, [(nc.scalar.copy, slice(0, N))])
         a = sb("a", [P, S], F32, "w2_raw")
         for h in range(2):
             nc.vector.tensor_copy(x_code[:, half(h)], word_table[:].bitcast(U32).indirect(entries(offs_sb, half(h))))
@@ -176,9 +172,10 @@ def tile_picked_box_p_kernel(
         for i in range(LISTS):
             nc.scalar.activation(rr_at[i][:], at(rr, i, every), ACT.Copy)
 
-        a0 = blocks("a0_", ("w3_raw", None))
+        a0_tile = sb("a0", [P, V], F32, "w1_grouped")
+        a0 = [a0_tile[:, block(b)] for b in range(BLOCKS)]
         for b in range(BLOCKS):
-            nc.vector.tensor_copy(a0[b][:], at(a, 0, block(b)))
+            nc.vector.tensor_copy(a0[b], at(a, 0, block(b)))
         a01 = fetch_with("a01_", a, 1, a0, ALU.add)
         den = fetch_with("den", a, 2, a01, ALU.add)
         ya = sb("ya", [P, S], F32, "a01_0")

@@ -63,14 +63,20 @@ def tile_picked_box_p_kernel(
             nc.sync.dma_start(tile[:], pos)
             return tile
 
+        def interleave_columns(copy, grouped, raw, cols):
+            copy(
+                grouped[:, cols, :].rearrange("p (c i) j -> p c j i", i=RUN),
+                raw[:, :, cols].rearrange("p j (c i) -> p c j i", i=RUN),
+            )
+
         def interleave(name, raw, shares, tag=None):
             grouped = sb(name + "_grouped", [P, N, PACK], BF16, tag)
             for copy, cols in shares:
-                copy(
-                    grouped[:, cols, :].rearrange("p (c i) j -> p c j i", i=RUN),
-                    raw[:, :, cols].rearrange("p j (c i) -> p c j i", i=RUN),
-                )
+                interleave_columns(copy, grouped, raw, cols)
             return grouped
+
+        def scalar_copy(dst, src):
+            nc.scalar.activation(dst, src, ACT.Identity, bias=copy_bias[:])
 
         on_vector = [(nc.vector.tensor_copy, slice(0, N))]
 
@@ -128,6 +134,7 @@ def tile_picked_box_p_kernel(
 
         x_scale = sb("x_scale", [P, S], U8)
         nc.gpsimd.memset(x_scale[:].bitcast(I32), 0)
+        copy_bias = zero_column("copy_bias")
         warm = sb("warm", [P, 1], F32)
         nc.scalar.activation(warm[:], zero[:], ACT.Exp)
 
@@ -144,8 +151,8 @@ def tile_picked_box_p_kernel(
         pt_sb = sb("pt_sb", [P, V], F32, "scale_picked")
         nc.sync.dma_start(pt_sb[:], pt)
 
-        w2_grouped = interleave("w2", w2_raw, [(nc.scalar.copy, slice(0, N))])
-        a = sb("a", [P, S], F32, "w2_raw")
+        w2_grouped = interleave("w2", w2_raw, [(scalar_copy, slice(0, N // 2)), (nc.scalar.copy, slice(N // 2, N))])
+        a = sb("a", [P, S], F32, "copy_bias")
         for h in range(2):
             nc.vector.tensor_copy(x_code[:, half(h)], word_table[:].bitcast(U32).indirect(entries(offs_sb, half(h))))
             for c in range(h * HALF // P, (h + 1) * HALF // P):
@@ -172,7 +179,7 @@ def tile_picked_box_p_kernel(
         for i in range(LISTS):
             nc.scalar.activation(rr_at[i][:], at(rr, i, every), ACT.Copy)
 
-        a0_tile = sb("a0", [P, V], F32, "w1_grouped")
+        a0_tile = sb("a0", [P, V], F32, "w3_raw")
         a0 = [a0_tile[:, block(b)] for b in range(BLOCKS)]
         for b in range(BLOCKS):
             nc.vector.tensor_copy(a0[b], at(a, 0, block(b)))

@@ -153,13 +153,12 @@ def tile_picked_box_p_kernel(
 
         w2_grouped = interleave("w2", w2_raw, [(scalar_copy, slice(0, N // 2)), (nc.scalar.copy, slice(N // 2, N))])
         a = sb("a", [P, S], F32, "copy_bias")
-        for h in range(2):
-            nc.vector.tensor_copy(x_code[:, half(h)], word_table[:].bitcast(U32).indirect(entries(offs_sb, half(h))))
-            for c in range(h * HALF // P, (h + 1) * HALF // P):
-                cols = slice(c * P, (c + 1) * P)
-                logits = bank("logits%d" % c)
-                product(logits[:, :P], w3_mx, cols)
-                nc.scalar.activation(a[:, cols], logits[:, :P], ACT.Exp, bias=zero[:])
+        for c in range(S // P):
+            cols = slice(c * P, (c + 1) * P)
+            nc.vector.tensor_copy(x_code[:, cols], word_table[:].bitcast(U32).indirect(entries(offs_sb, cols)))
+            logits = bank("logits%d" % c)
+            product(logits[:, :P], w3_mx, cols)
+            nc.scalar.activation(a[:, cols], logits[:, :P], ACT.Exp, bias=zero[:])
 
         w2_mx = quantize("w2", w2_grouped)
         w1_grouped = interleave("w1", w1_raw, on_vector)
@@ -172,38 +171,41 @@ def tile_picked_box_p_kernel(
             product(y[h][:, :HALF], w1_mx, half(h))
         every = slice(0, V)
 
-        rr = sb("rr", [P, S], F32, "zero")
-        for h in range(2):
-            nc.scalar.activation(rr[:, half(h)], r[h][:, :HALF], ACT.Relu)
+        rr = sb("rr", [P, S], F32, "w3_raw")
+        nc.vector.tensor_scalar_max(rr[:, half(0)], r[0][:, :HALF], 0.0)
+        nc.scalar.activation(rr[:, half(1)], r[1][:, :HALF], ACT.Relu)
+        a0_tile = sb("a0", [P, V], F32, "w1_grouped")
+        a0 = [a0_tile[:, block(b)] for b in range(BLOCKS)]
+        nc.vector.tensor_copy(a0[0], at(a, 0, block(0)))
+        nc.scalar.activation(a0[1], at(a, 0, block(1)), ACT.Copy)
         rr_at = [sb("rr_at%d" % i, [P, V], F32) for i in range(LISTS)]
         for i in range(LISTS):
             nc.scalar.activation(rr_at[i][:], at(rr, i, every), ACT.Copy)
 
-        a0_tile = sb("a0", [P, V], F32, "w3_raw")
-        a0 = [a0_tile[:, block(b)] for b in range(BLOCKS)]
-        for b in range(BLOCKS):
-            nc.vector.tensor_copy(a0[b], at(a, 0, block(b)))
-        a01 = fetch_with("a01_", a, 1, a0, ALU.add)
-        den = fetch_with("den", a, 2, a01, ALU.add)
-        ya = sb("ya", [P, S], F32, "a01_0")
+        ya = sb("ya", [P, S], F32)
         for h in range(2):
             nc.vector.tensor_tensor(ya[:, half(h)], y[h][:, :HALF], a[:, half(h)], ALU.mult)
-        pt_den = blocks("pt_den")
+        a01 = fetch_with("a01_", a, 1, a0, ALU.add)
+        den_tile = sb("den", [P, V], F32)
+        den = [den_tile[:, block(b)] for b in range(BLOCKS)]
         for b in range(BLOCKS):
-            nc.gpsimd.tensor_tensor(pt_den[b][:], pt_sb[:, block(b)], den[b][:], ALU.mult)
+            nc.vector.tensor_tensor(den[b], at(a, 2, block(b)), a01[b][:], ALU.add)
+        off01 = sb("off01", [P, V], F32, "a01_0")
+        nc.vector.tensor_tensor(off01[:], rr_at[0][:], rr_at[1][:], ALU.min)
+        pt_den_tile = sb("pt_den", [P, V], F32)
+        nc.vector.tensor_tensor(pt_den_tile[:], pt_sb[:], den_tile[:], ALU.mult)
+        pt_den = [pt_den_tile[:, block(b)] for b in range(BLOCKS)]
+        off = sb("off", [P, V], F32)
+        nc.vector.tensor_tensor(off[:], off01[:], rr_at[2][:], ALU.min)
 
-        root = sb("root", [P, V], F32, "zero")
+        root = sb("root", [P, V], F32, "w3_raw")
         for b in range(BLOCKS):
             nc.scalar.activation(root[:, block(b)], den[b][:], ACT.Abs_reciprocal_sqrt)
         rec = blocks("rec")
         for b in range(BLOCKS):
             nc.scalar.activation(rec[b][:], root[:, block(b)], ACT.Square)
 
-        off01 = sb("off01", [P, V], F32, "a01_1")
-        nc.vector.tensor_tensor(off01[:], rr_at[0][:], rr_at[1][:], ALU.min)
         gap0 = fetch_with("gap0_", ya, 0, pt_den, ALU.subtract)
-        off = sb("off", [P, V], F32, "pt_den0")
-        nc.vector.tensor_tensor(off[:], off01[:], rr_at[2][:], ALU.min)
         gap01 = fetch_with("gap01_", ya, 1, gap0, ALU.add)
         gap = fetch_with("gap", ya, 2, gap01, ALU.add)
         size = blocks("size")

@@ -63,20 +63,14 @@ def tile_picked_box_p_kernel(
             nc.sync.dma_start(tile[:], pos)
             return tile
 
-        def interleave_columns(copy, grouped, raw, cols):
-            copy(
-                grouped[:, cols, :].rearrange("p (c i) j -> p c j i", i=RUN),
-                raw[:, :, cols].rearrange("p j (c i) -> p c j i", i=RUN),
-            )
-
         def interleave(name, raw, shares, tag=None):
             grouped = sb(name + "_grouped", [P, N, PACK], BF16, tag)
             for copy, cols in shares:
-                interleave_columns(copy, grouped, raw, cols)
+                copy(
+                    grouped[:, cols, :].rearrange("p (c i) j -> p c j i", i=RUN),
+                    raw[:, :, cols].rearrange("p j (c i) -> p c j i", i=RUN),
+                )
             return grouped
-
-        def scalar_copy(dst, src):
-            nc.scalar.activation(dst, src, ACT.Identity, bias=copy_bias[:])
 
         on_vector = [(nc.vector.tensor_copy, slice(0, N))]
 
@@ -134,7 +128,6 @@ def tile_picked_box_p_kernel(
 
         x_scale = sb("x_scale", [P, S], U8)
         nc.gpsimd.memset(x_scale[:].bitcast(I32), 0)
-        copy_bias = zero_column("copy_bias")
         warm = sb("warm", [P, 1], F32)
         nc.scalar.activation(warm[:], zero[:], ACT.Exp)
 
@@ -151,14 +144,15 @@ def tile_picked_box_p_kernel(
         pt_sb = sb("pt_sb", [P, V], F32, "scale_picked")
         nc.sync.dma_start(pt_sb[:], pt)
 
-        w2_grouped = interleave("w2", w2_raw, [(scalar_copy, slice(0, N // 2)), (nc.scalar.copy, slice(N // 2, N))])
-        a = sb("a", [P, S], F32, "copy_bias")
-        for c in range(S // P):
-            cols = slice(c * P, (c + 1) * P)
-            nc.vector.tensor_copy(x_code[:, cols], word_table[:].bitcast(U32).indirect(entries(offs_sb, cols)))
-            logits = bank("logits%d" % c)
-            product(logits[:, :P], w3_mx, cols)
-            nc.scalar.activation(a[:, cols], logits[:, :P], ACT.Exp, bias=zero[:])
+        w2_grouped = interleave("w2", w2_raw, [(nc.scalar.copy, slice(0, N))])
+        a = sb("a", [P, S], F32, "w2_raw")
+        for h in range(2):
+            nc.vector.tensor_copy(x_code[:, half(h)], word_table[:].bitcast(U32).indirect(entries(offs_sb, half(h))))
+            for c in range(h * HALF // P, (h + 1) * HALF // P):
+                cols = slice(c * P, (c + 1) * P)
+                logits = bank("logits%d" % c)
+                product(logits[:, :P], w3_mx, cols)
+                nc.scalar.activation(a[:, cols], logits[:, :P], ACT.Exp, bias=zero[:])
 
         w2_mx = quantize("w2", w2_grouped)
         w1_grouped = interleave("w1", w1_raw, on_vector)
@@ -166,31 +160,29 @@ def tile_picked_box_p_kernel(
         for h in range(2):
             product(r[h][:, :HALF], w2_mx, half(h))
         w1_mx = quantize("w1", w1_grouped, "w2_grouped")
-        y = [bank("y%d" % h) for h in range(2)]
+        y = [bank(name) for name in ("y0", "r1")]
         for h in range(2):
             product(y[h][:, :HALF], w1_mx, half(h))
         every = slice(0, V)
 
-        rr = sb("rr", [P, S], F32, "w3_raw")
-        nc.vector.tensor_scalar_max(rr[:, half(0)], r[0][:, :HALF], 0.0)
-        nc.scalar.activation(rr[:, half(1)], r[1][:, :HALF], ACT.Relu)
+        rr = sb("rr", [P, S], F32, "zero")
+        for h in range(2):
+            nc.scalar.activation(rr[:, half(h)], r[h][:, :HALF], ACT.Relu)
         a0_tile = sb("a0", [P, V], F32, "w1_grouped")
-        a0 = [a0_tile[:, block(b)] for b in range(BLOCKS)]
-        nc.vector.tensor_copy(a0[0], at(a, 0, block(0)))
-        nc.scalar.activation(a0[1], at(a, 0, block(1)), ACT.Copy)
+        nc.vector.tensor_copy(a0_tile[:], at(a, 0, every))
         rr_at = [sb("rr_at%d" % i, [P, V], F32) for i in range(LISTS)]
         for i in range(LISTS):
             nc.scalar.activation(rr_at[i][:], at(rr, i, every), ACT.Copy)
 
         ya = sb("ya", [P, S], F32)
-        for h in range(2):
-            nc.vector.tensor_tensor(ya[:, half(h)], y[h][:, :HALF], a[:, half(h)], ALU.mult)
-        a01 = fetch_with("a01_", a, 1, a0, ALU.add)
+        nc.vector.tensor_tensor(ya[:, half(0)], y[0][:, :HALF], a[:, half(0)], ALU.mult)
+        a01 = sb("a01", [P, V], F32)
+        nc.vector.tensor_tensor(a01[:], at(a, 1, every), a0_tile[:], ALU.add)
+        nc.vector.tensor_tensor(ya[:, half(1)], y[1][:, :HALF], a[:, half(1)], ALU.mult)
         den_tile = sb("den", [P, V], F32)
         den = [den_tile[:, block(b)] for b in range(BLOCKS)]
-        for b in range(BLOCKS):
-            nc.vector.tensor_tensor(den[b], at(a, 2, block(b)), a01[b][:], ALU.add)
-        off01 = sb("off01", [P, V], F32, "a01_0")
+        nc.vector.tensor_tensor(den_tile[:], at(a, 2, every), a01[:], ALU.add)
+        off01 = sb("off01", [P, V], F32, "w1_grouped")
         nc.vector.tensor_tensor(off01[:], rr_at[0][:], rr_at[1][:], ALU.min)
         pt_den_tile = sb("pt_den", [P, V], F32)
         nc.vector.tensor_tensor(pt_den_tile[:], pt_sb[:], den_tile[:], ALU.mult)
@@ -198,7 +190,7 @@ def tile_picked_box_p_kernel(
         off = sb("off", [P, V], F32)
         nc.vector.tensor_tensor(off[:], off01[:], rr_at[2][:], ALU.min)
 
-        root = sb("root", [P, V], F32, "w3_raw")
+        root = sb("root", [P, V], F32, "zero")
         for b in range(BLOCKS):
             nc.scalar.activation(root[:, block(b)], den[b][:], ACT.Abs_reciprocal_sqrt)
         rec = blocks("rec")

@@ -24,6 +24,7 @@ ROWS = 4
 BANK = 512
 LISTS = 3
 HALF = S // 2
+PIECE = 128
 BLOCKS = 2
 WIDTH = V // BLOCKS
 STAGE_END = P // 2
@@ -63,16 +64,13 @@ def tile_picked_box_p_kernel(
             nc.sync.dma_start(tile[:], pos)
             return tile
 
-        def interleave(name, raw, shares, tag=None):
+        def interleave(name, raw, copy, tag=None):
             grouped = sb(name + "_grouped", [P, N, PACK], BF16, tag)
-            for copy, cols in shares:
-                copy(
-                    grouped[:, cols, :].rearrange("p (c i) j -> p c j i", i=RUN),
-                    raw[:, :, cols].rearrange("p j (c i) -> p c j i", i=RUN),
-                )
+            copy(
+                grouped[:].rearrange("p (c i) j -> p c j i", i=RUN),
+                raw[:].rearrange("p j (c i) -> p c j i", i=RUN),
+            )
             return grouped
-
-        on_vector = [(nc.vector.tensor_copy, slice(0, N))]
 
         def quantize(name, grouped, tag=None):
             codes = sb(name + "_codes", [P, N], U32, tag)
@@ -94,24 +92,22 @@ def tile_picked_box_p_kernel(
                 stop=True,
             )
 
-        def blocks(name, tags=(None, None)):
-            return [sb("%s%d" % (name, b), [P, WIDTH], F32, tags[b]) for b in range(BLOCKS)]
+        def blocks(name):
+            return [sb("%s%d" % (name, b), [P, WIDTH], F32) for b in range(BLOCKS)]
 
-        def at(table, i, cols):
-            return table[:].indirect(entries(pos_sb[i], cols))
+        def at(table, i, queries):
+            return table[:].indirect(entries(pos_sb[i], queries))
 
-        def fetch_with(name, table, i, partial, op, tags=(None, None)):
-            total = blocks(name, tags)
+        def fetch_with(name, table, i, partial, op):
+            total = blocks(name)
             for b in range(BLOCKS):
-                nc.vector.tensor_tensor(total[b][:], at(table, i, block(b)), partial[b][:], op)
-            return total
+                nc.vector.tensor_tensor(total[b][:], at(table, i, block(b)), partial[b], op)
+            return [tile[:] for tile in total]
 
-        def zero_column(name):
-            column = sb(name, [P, 1], F32)
-            nc.gpsimd.memset(column[:], 0.0)
-            return column
+        every = slice(0, V)
 
-        zero = zero_column("zero")
+        zero = sb("zero", [P, 1], F32)
+        nc.gpsimd.memset(zero[:], 0.0)
 
         scale_table = sb("scale_table", [P, T], U8)
         nc.gpsimd.memset(scale_table[0:STAGE, :].bitcast(I32), 0)
@@ -133,7 +129,7 @@ def tile_picked_box_p_kernel(
 
         scale_picked = sb("scale_picked", [P, S], U8)
         nc.vector.tensor_copy(scale_picked[:], scale_table[:].indirect(offs_sb[:]))
-        w3_grouped = interleave("w3", w3_raw, on_vector, "scale_table")
+        w3_grouped = interleave("w3", w3_raw, nc.vector.tensor_copy, "scale_table")
         w3_mx = quantize("w3", w3_grouped)
         w1_raw = load_weight("w1", w1, "w3_raw")
         x_code = sb("x_code", [P, S], U32, "scale_table")
@@ -144,32 +140,32 @@ def tile_picked_box_p_kernel(
         pt_sb = sb("pt_sb", [P, V], F32, "scale_picked")
         nc.sync.dma_start(pt_sb[:], pt)
 
-        w2_grouped = interleave("w2", w2_raw, [(nc.scalar.copy, slice(0, N))])
+        w2_grouped = interleave("w2", w2_raw, nc.scalar.copy)
         a = sb("a", [P, S], F32, "w2_raw")
-        for h in range(2):
+        for h in range(S // HALF):
             nc.vector.tensor_copy(x_code[:, half(h)], word_table[:].bitcast(U32).indirect(entries(offs_sb, half(h))))
-            for c in range(h * HALF // P, (h + 1) * HALF // P):
-                cols = slice(c * P, (c + 1) * P)
+            for c in range(h * HALF // PIECE, (h + 1) * HALF // PIECE):
+                cols = slice(c * PIECE, (c + 1) * PIECE)
                 logits = bank("logits%d" % c)
-                product(logits[:, :P], w3_mx, cols)
-                nc.scalar.activation(a[:, cols], logits[:, :P], ACT.Exp, bias=zero[:])
+                product(logits[:, :PIECE], w3_mx, cols)
+                nc.scalar.activation(a[:, cols], logits[:, :PIECE], ACT.Exp, bias=zero[:] if cols.stop < S else 0.0)
 
         w2_mx = quantize("w2", w2_grouped)
-        w1_grouped = interleave("w1", w1_raw, on_vector)
-        r = [bank("r%d" % h) for h in range(2)]
-        for h in range(2):
+        w1_grouped = interleave("w1", w1_raw, nc.vector.tensor_copy)
+        r = [bank("r%d" % h) for h in range(S // HALF)]
+        for h in range(S // HALF):
             product(r[h][:, :HALF], w2_mx, half(h))
         w1_mx = quantize("w1", w1_grouped, "w2_grouped")
         y = [bank(name) for name in ("y0", "r1")]
-        for h in range(2):
+        for h in range(S // HALF):
             product(y[h][:, :HALF], w1_mx, half(h))
-        every = slice(0, V)
 
         rr = sb("rr", [P, S], F32, "zero")
-        for h in range(2):
+        for h in range(S // HALF):
             nc.scalar.activation(rr[:, half(h)], r[h][:, :HALF], ACT.Relu)
-        a0_tile = sb("a0", [P, V], F32, "w1_grouped")
-        nc.vector.tensor_copy(a0_tile[:], at(a, 0, every))
+        a0 = sb("a0", [P, V], F32, "w1_grouped")
+        nc.vector.tensor_copy(a0[:, block(0)], at(a, 0, block(0)))
+        nc.scalar.activation(a0[:, block(1)], at(a, 0, block(1)), ACT.Copy)
         rr_at = [sb("rr_at%d" % i, [P, V], F32) for i in range(LISTS)]
         for i in range(LISTS):
             nc.scalar.activation(rr_at[i][:], at(rr, i, every), ACT.Copy)
@@ -177,36 +173,35 @@ def tile_picked_box_p_kernel(
         ya = sb("ya", [P, S], F32)
         nc.vector.tensor_tensor(ya[:, half(0)], y[0][:, :HALF], a[:, half(0)], ALU.mult)
         a01 = sb("a01", [P, V], F32)
-        nc.vector.tensor_tensor(a01[:], at(a, 1, every), a0_tile[:], ALU.add)
+        for b in range(BLOCKS):
+            nc.vector.tensor_tensor(a01[:, block(b)], at(a, 1, block(b)), a0[:, block(b)], ALU.add)
         nc.vector.tensor_tensor(ya[:, half(1)], y[1][:, :HALF], a[:, half(1)], ALU.mult)
-        den_tile = sb("den", [P, V], F32)
-        den = [den_tile[:, block(b)] for b in range(BLOCKS)]
-        nc.vector.tensor_tensor(den_tile[:], at(a, 2, every), a01[:], ALU.add)
+        den = sb("den", [P, V], F32)
+        nc.vector.tensor_tensor(den[:], at(a, 2, every), a01[:], ALU.add)
         off01 = sb("off01", [P, V], F32, "w1_grouped")
         nc.vector.tensor_tensor(off01[:], rr_at[0][:], rr_at[1][:], ALU.min)
-        pt_den_tile = sb("pt_den", [P, V], F32)
-        nc.vector.tensor_tensor(pt_den_tile[:], pt_sb[:], den_tile[:], ALU.mult)
-        pt_den = [pt_den_tile[:, block(b)] for b in range(BLOCKS)]
+        pt_den = sb("pt_den", [P, V], F32)
+        nc.vector.tensor_tensor(pt_den[:], pt_sb[:], den[:], ALU.mult)
         off = sb("off", [P, V], F32)
         nc.vector.tensor_tensor(off[:], off01[:], rr_at[2][:], ALU.min)
 
         root = sb("root", [P, V], F32, "zero")
         for b in range(BLOCKS):
-            nc.scalar.activation(root[:, block(b)], den[b][:], ACT.Abs_reciprocal_sqrt)
+            nc.scalar.activation(root[:, block(b)], den[:, block(b)], ACT.Abs_reciprocal_sqrt)
         rec = blocks("rec")
         for b in range(BLOCKS):
             nc.scalar.activation(rec[b][:], root[:, block(b)], ACT.Square)
 
-        gap0 = fetch_with("gap0_", ya, 0, pt_den, ALU.subtract)
+        gap0 = fetch_with("gap0_", ya, 0, [pt_den[:, block(b)] for b in range(BLOCKS)], ALU.subtract)
         gap01 = fetch_with("gap01_", ya, 1, gap0, ALU.add)
         gap = fetch_with("gap", ya, 2, gap01, ALU.add)
         size = blocks("size")
         for b in range(BLOCKS):
-            nc.scalar.activation(size[b][:], gap[b][:], ACT.Abs)
+            nc.scalar.activation(size[b][:], gap[b], ACT.Abs)
 
         off_den = sb("off_den", [P, V], F32, "gap01_0")
         for b in range(BLOCKS):
-            nc.vector.tensor_tensor(off_den[:, block(b)], off[:, block(b)], den[b][:], ALU.mult)
+            nc.vector.tensor_tensor(off_den[:, block(b)], off[:, block(b)], den[:, block(b)], ALU.mult)
         beyond = blocks("beyond")
         for b in range(BLOCKS):
             nc.vector.tensor_tensor(beyond[b][:], size[b][:], off_den[:, block(b)], ALU.subtract)

@@ -148,7 +148,7 @@ def tile_picked_box_p_kernel(
                 cols = slice(c * PIECE, (c + 1) * PIECE)
                 logits = bank("logits%d" % c)
                 product(logits[:, :PIECE], w3_mx, cols)
-                nc.scalar.activation(a[:, cols], logits[:, :PIECE], ACT.Exp, bias=zero[:] if cols.stop < S else 0.0)
+                nc.scalar.activation(a[:, cols], logits[:, :PIECE], ACT.Exp, bias=zero[:])
 
         w2_mx = quantize("w2", w2_grouped)
         w1_grouped = interleave("w1", w1_raw, nc.vector.tensor_copy)
@@ -160,9 +160,9 @@ def tile_picked_box_p_kernel(
         for h in range(S // HALF):
             product(y[h][:, :HALF], w1_mx, half(h))
 
-        rr = sb("rr", [P, S], F32, "zero")
-        for h in range(S // HALF):
-            nc.scalar.activation(rr[:, half(h)], r[h][:, :HALF], ACT.Relu)
+        rr = sb("rr", [P, S], F32, "w3_raw")
+        nc.vector.tensor_scalar_max(rr[:, half(0)], r[0][:, :HALF], 0.0)
+        nc.scalar.activation(rr[:, half(1)], r[1][:, :HALF], ACT.Relu)
         a0 = sb("a0", [P, V], F32, "w1_grouped")
         nc.vector.tensor_copy(a0[:, block(0)], at(a, 0, block(0)))
         nc.scalar.activation(a0[:, block(1)], at(a, 0, block(1)), ACT.Copy)
@@ -185,7 +185,7 @@ def tile_picked_box_p_kernel(
         off = sb("off", [P, V], F32)
         nc.vector.tensor_tensor(off[:], off01[:], rr_at[2][:], ALU.min)
 
-        root = sb("root", [P, V], F32, "zero")
+        root = sb("root", [P, V], F32, "w3_raw")
         for b in range(BLOCKS):
             nc.scalar.activation(root[:, block(b)], den[:, block(b)], ACT.Abs_reciprocal_sqrt)
         rec = blocks("rec")

@@ -37,10 +37,14 @@ def tile_picked_box_p_kernel(
     nc = tc.nc
     with ExitStack() as ctx:
         keep = ctx.enter_context(tc.tile_pool(name="keep", bufs=1))
+        placed = ctx.enter_context(tc.tile_pool(name="placed", bufs=1))
         psum = ctx.enter_context(tc.psum_pool(name="psum", bufs=1))
 
         def sb(name, shape, dtype, tag=None):
             return keep.tile(shape, dtype, name=name, tag=tag or name, align_bytes=64)
+
+        def place(name, shape, dtype, offset):
+            return placed.tile(shape, dtype, name=name, tag=name, align_bytes=64, offset=offset)
 
         def bank(name):
             return psum.tile([P, BANK], F32, name=name, tag=name)
@@ -64,8 +68,7 @@ def tile_picked_box_p_kernel(
             nc.sync.dma_start(tile[:], pos)
             return tile
 
-        def interleave(name, raw, copy, tag=None):
-            grouped = sb(name + "_grouped", [P, N, PACK], BF16, tag)
+        def interleave(grouped, raw, copy):
             copy(
                 grouped[:].rearrange("p (c i) j -> p c j i", i=RUN),
                 raw[:].rearrange("p j (c i) -> p c j i", i=RUN),
@@ -129,7 +132,7 @@ def tile_picked_box_p_kernel(
 
         scale_picked = sb("scale_picked", [P, S], U8)
         nc.vector.tensor_copy(scale_picked[:], scale_table[:].indirect(offs_sb[:]))
-        w3_grouped = interleave("w3", w3_raw, nc.vector.tensor_copy, "scale_table")
+        w3_grouped = interleave(sb("w3_grouped", [P, N, PACK], BF16, "scale_table"), w3_raw, nc.vector.tensor_copy)
         w3_mx = quantize("w3", w3_grouped)
         w1_raw = load_weight("w1", w1, "w3_raw")
         x_code = sb("x_code", [P, S], U32, "scale_table")
@@ -140,7 +143,7 @@ def tile_picked_box_p_kernel(
         pt_sb = sb("pt_sb", [P, V], F32, "scale_picked")
         nc.sync.dma_start(pt_sb[:], pt)
 
-        w2_grouped = interleave("w2", w2_raw, nc.scalar.copy)
+        w2_grouped = interleave(sb("w2_grouped", [P, N, PACK], BF16), w2_raw, nc.scalar.copy)
         a = sb("a", [P, S], F32, "w2_raw")
         for h in range(S // HALF):
             nc.vector.tensor_copy(x_code[:, half(h)], word_table[:].bitcast(U32).indirect(entries(offs_sb, half(h))))
@@ -151,56 +154,60 @@ def tile_picked_box_p_kernel(
                 nc.scalar.activation(a[:, cols], logits[:, :PIECE], ACT.Exp, bias=zero[:])
 
         w2_mx = quantize("w2", w2_grouped)
-        w1_grouped = interleave("w1", w1_raw, nc.vector.tensor_copy)
+        w1_grouped = interleave(place("w1_grouped", [P, N, PACK], BF16, 1024), w1_raw, nc.vector.tensor_copy)
         r = [bank("r%d" % h) for h in range(S // HALF)]
         for h in range(S // HALF):
             product(r[h][:, :HALF], w2_mx, half(h))
         w1_mx = quantize("w1", w1_grouped, "w2_grouped")
-        y = [bank(name) for name in ("y0", "r1")]
+        y = [bank(name) for name in ("y0", "y1")]
         for h in range(S // HALF):
             product(y[h][:, :HALF], w1_mx, half(h))
 
         rr = sb("rr", [P, S], F32, "w3_raw")
         nc.vector.tensor_scalar_max(rr[:, half(0)], r[0][:, :HALF], 0.0)
         nc.scalar.activation(rr[:, half(1)], r[1][:, :HALF], ACT.Relu)
-        a0 = sb("a0", [P, V], F32, "w1_grouped")
-        nc.vector.tensor_copy(a0[:, block(0)], at(a, 0, block(0)))
-        nc.scalar.activation(a0[:, block(1)], at(a, 0, block(1)), ACT.Copy)
-        rr_at = [sb("rr_at%d" % i, [P, V], F32) for i in range(LISTS)]
-        for i in range(LISTS):
-            nc.scalar.activation(rr_at[i][:], at(rr, i, every), ACT.Copy)
-
+        a0 = [place("a0_0", [P, WIDTH], F32, 1536), place("a0_1", [P, WIDTH], F32, 1024)]
+        nc.vector.tensor_copy(a0[0][:], at(a, 0, block(0)))
+        nc.scalar.activation(a0[1][:], at(a, 0, block(1)), ACT.Copy)
+        rr_at = [sb("rr_at0", [P, V], F32), place("rr_at1", [P, V], F32, 1792), place("rr_at2", [P, V], F32, 768)]
+        nc.scalar.activation(rr_at[0][:], at(rr, 0, every), ACT.Copy)
         ya = sb("ya", [P, S], F32)
-        nc.vector.tensor_tensor(ya[:, half(0)], y[0][:, :HALF], a[:, half(0)], ALU.mult)
+        for h in range(S // HALF):
+            nc.vector.tensor_tensor(ya[:, half(h)], y[h][:, :HALF], a[:, half(h)], ALU.mult)
+        num0 = sb("num0", [P, V], F32)
+        nc.scalar.activation(num0[:], at(ya, 0, every), ACT.Copy)
         a01 = sb("a01", [P, V], F32)
         for b in range(BLOCKS):
-            nc.vector.tensor_tensor(a01[:, block(b)], at(a, 1, block(b)), a0[:, block(b)], ALU.add)
-        nc.vector.tensor_tensor(ya[:, half(1)], y[1][:, :HALF], a[:, half(1)], ALU.mult)
+            nc.vector.tensor_tensor(a01[:, block(b)], at(a, 1, block(b)), a0[b][:], ALU.add)
+        for i in range(1, LISTS):
+            nc.scalar.activation(rr_at[i][:], at(rr, i, every), ACT.Copy)
         den = sb("den", [P, V], F32)
-        nc.vector.tensor_tensor(den[:], at(a, 2, every), a01[:], ALU.add)
-        off01 = sb("off01", [P, V], F32, "w1_grouped")
-        nc.vector.tensor_tensor(off01[:], rr_at[0][:], rr_at[1][:], ALU.min)
+        for b in range(BLOCKS):
+            nc.vector.tensor_tensor(den[:, block(b)], at(a, 2, block(b)), a01[:, block(b)], ALU.add)
+        num01 = sb("num01", [P, V], F32)
+        nc.vector.tensor_tensor(num01[:], at(ya, 1, every), num0[:], ALU.add)
         pt_den = sb("pt_den", [P, V], F32)
         nc.vector.tensor_tensor(pt_den[:], pt_sb[:], den[:], ALU.mult)
+        off01 = sb("off01", [P, V], F32, "a01")
+        nc.vector.tensor_tensor(off01[:], rr_at[0][:], rr_at[1][:], ALU.min)
+        gap01 = sb("gap01", [P, V], F32)
+        nc.vector.tensor_tensor(gap01[:], num01[:], pt_den[:], ALU.subtract)
         off = sb("off", [P, V], F32)
         nc.vector.tensor_tensor(off[:], off01[:], rr_at[2][:], ALU.min)
 
         root = sb("root", [P, V], F32, "w3_raw")
         for b in range(BLOCKS):
             nc.scalar.activation(root[:, block(b)], den[:, block(b)], ACT.Abs_reciprocal_sqrt)
+
+        gap = fetch_with("gap", ya, 2, [gap01[:, block(b)] for b in range(BLOCKS)], ALU.add)
         rec = blocks("rec")
         for b in range(BLOCKS):
             nc.scalar.activation(rec[b][:], root[:, block(b)], ACT.Square)
 
-        gap0 = fetch_with("gap0_", ya, 0, [pt_den[:, block(b)] for b in range(BLOCKS)], ALU.subtract)
-        gap01 = fetch_with("gap01_", ya, 1, gap0, ALU.add)
-        gap = fetch_with("gap", ya, 2, gap01, ALU.add)
         size = blocks("size")
+        off_den = sb("off_den", [P, V], F32, "num01")
         for b in range(BLOCKS):
-            nc.scalar.activation(size[b][:], gap[b], ACT.Abs)
-
-        off_den = sb("off_den", [P, V], F32, "gap01_0")
-        for b in range(BLOCKS):
+            nc.vector.scalar_tensor_tensor(size[b][:], gap[b], -1.0, gap[b], ALU.mult, ALU.max)
             nc.vector.tensor_tensor(off_den[:, block(b)], off[:, block(b)], den[:, block(b)], ALU.mult)
         beyond = blocks("beyond")
         for b in range(BLOCKS):

@@ -27,7 +27,7 @@ HALF = S // 2
 PIECE = 128
 BLOCKS = 2
 WIDTH = V // BLOCKS
-STAGE_END = P // 2
+STAGE_END = P
 STAGE = STAGE_END - K // QUADRANT
 
 
@@ -114,7 +114,6 @@ def tile_picked_box_p_kernel(
 
         scale_table = sb("scale_table", [P, T], U8)
         nc.gpsimd.memset(scale_table[0:STAGE, :].bitcast(I32), 0)
-        nc.gpsimd.memset(scale_table[STAGE_END:P, :].bitcast(I32), 0)
         nc.scalar.dma_start(scale_table[STAGE:STAGE_END, :].bitcast(I32), x_scales[0].bitcast(I32))
         offs_sb = sb("offs_sb", [P, S // GROUP], U16)
         nc.sync.dma_start(offs_sb[:], offs)

from contextlib import ExitStack

import concourse.mybir as mybir

K, T, S, V, N = 512, 2048, 512, 256, 128
FLOPS = 3 * 2 * K * N * S

F32 = mybir.dt.float32
BF16 = mybir.dt.bfloat16
I32 = mybir.dt.int32
U32 = mybir.dt.uint32
U16 = mybir.dt.uint16
U8 = mybir.dt.uint8
FP8X4 = mybir.dt.float8_e4m3fn_x4
ACT = mybir.ActivationFunctionType
ALU = mybir.AluOpType

P = 128
PACK = 4
RUN = 4
GROUP = 16
QUADRANT = 32
ROWS = 4
BANK = 512
LISTS = 3
HALF = S // 2
PIECE = 128
BLOCKS = 2
WIDTH = V // BLOCKS
STAGE_END = P
STAGE = STAGE_END - K // QUADRANT


def tile_picked_box_p_kernel(
    tc, x_words, x_scales, w1, w2, w3, pt, offs, pos1, pos2, pos3, out
):
    nc = tc.nc
    with ExitStack() as ctx:
        keep = ctx.enter_context(tc.tile_pool(name="keep", bufs=1))
        placed = ctx.enter_context(tc.tile_pool(name="placed", bufs=1))
        psum = ctx.enter_context(tc.psum_pool(name="psum", bufs=1))

        def sb(name, shape, dtype, tag=None):
            return keep.tile(shape, dtype, name=name, tag=tag or name, align_bytes=64)

        def place(name, shape, dtype, offset):
            return placed.tile(shape, dtype, name=name, tag=name, align_bytes=64, offset=offset)

        def bank(name):
            return psum.tile([P, BANK], F32, name=name, tag=name)

        def block(b):
            return slice(b * WIDTH, (b + 1) * WIDTH)

        def half(h):
            return slice(h * HALF, (h + 1) * HALF)

        def entries(list_tile, cols):
            return list_tile[:, cols.start // GROUP : cols.stop // GROUP]

        def load_weight(name, w, tag=None):
            raw = sb(name + "_raw", [P, PACK, N], F32, tag)
            nc.sync.dma_start(raw[:], w.rearrange("(p j) m -> p j m", j=PACK))
            return raw

        def load_list(i, pos):
            tile = sb("pos%d_sb" % i, [P, V // GROUP], U16)
            nc.sync.dma_start(tile[:], pos)
            return tile

        def interleave(grouped, raw, copy):
            copy(
                grouped[:].rearrange("p (c i) j -> p c j i", i=RUN),
                raw[:].rearrange("p j (c i) -> p c j i", i=RUN),
            )
            return grouped

        def quantize(name, grouped, tag=None):
            codes = sb(name + "_codes", [P, N], U32, tag)
            scales = sb(name + "_scales", [P, N], U8)
            nc.vector.quantize_mx(
                out=codes[:].bitcast(FP8X4), scales=scales[:], in_=grouped[:].rearrange("p m j -> p (m j)")
            )
            return codes, scales

        def product(acc, weight, cols):
            codes, scales = weight
            nc.tensor.matmul_mx(
                out=acc,
                lhsT=codes[:].bitcast(FP8X4),
                lhsT_scale=scales[:],
                rhs=x_code[:, cols].bitcast(FP8X4),
                rhs_scale=x_scale[:, cols],
                start=True,
                stop=True,
            )

        def blocks(name):
            return [sb("%s%d" % (name, b), [P, WIDTH], F32) for b in range(BLOCKS)]

        def at(table, i, queries):
            return table[:].indirect(entries(pos_sb[i], queries))

        def fetch_with(name, table, i, partial, op):
            total = blocks(name)
            for b in range(BLOCKS):
                nc.vector.tensor_tensor(total[b][:], at(table, i, block(b)), partial[b], op)
            return [tile[:] for tile in total]

        every = slice(0, V)

        zero = sb("zero", [P, 1], F32)
        nc.gpsimd.memset(zero[:], 0.0)

        scale_table = sb("scale_table", [P, T], U8)
        nc.gpsimd.memset(scale_table[0:STAGE, :].bitcast(I32), 0)
        nc.scalar.dma_start(scale_table[STAGE:STAGE_END, :].bitcast(I32), x_scales[0].bitcast(I32))
        offs_sb = sb("offs_sb", [P, S // GROUP], U16)
        nc.sync.dma_start(offs_sb[:], offs)
        w3_raw = load_weight("w3", w3)
        pos_sb = [load_list(i, pos) for i, pos in enumerate((pos1, pos2))]
        word_table = sb("word_table", [P, T], I32)
        nc.sync.dma_start(word_table[:], x_words[0].rearrange("p n t -> p (n t)").bitcast(I32))
        w2_raw = load_weight("w2", w2)
        pos_sb.append(load_list(LISTS - 1, pos3))

        x_scale = sb("x_scale", [P, S], U8)
        nc.gpsimd.memset(x_scale[:].bitcast(I32), 0)
        warm = sb("warm", [P, 1], F32)
        nc.scalar.activation(warm[:], zero[:], ACT.Exp)

        scale_picked = sb("scale_picked", [P, S], U8)
        nc.vector.tensor_copy(scale_picked[:], scale_table[:].indirect(offs_sb[:]))
        w3_grouped = interleave(sb("w3_grouped", [P, N, PACK], BF16, "scale_table"), w3_raw, nc.vector.tensor_copy)
        w3_mx = quantize("w3", w3_grouped)
        w1_raw = load_weight("w1", w1, "w3_raw")
        x_code = sb("x_code", [P, S], U32, "scale_table")
        for j in range(ROWS):
            nc.scalar.dma_start(
                x_scale[j:P:QUADRANT, :].bitcast(I32), scale_picked[STAGE + j : STAGE_END : ROWS, :].bitcast(I32)
            )
        pt_sb = sb("pt_sb", [P, V], F32, "scale_picked")
        nc.sync.dma_start(pt_sb[:], pt)

        w2_grouped = interleave(sb("w2_grouped", [P, N, PACK], BF16), w2_raw, nc.scalar.copy)
        a = sb("a", [P, S], F32, "w2_raw")
        for h in range(S // HALF):
            nc.vector.tensor_copy(x_code[:, half(h)], word_table[:].bitcast(U32).indirect(entries(offs_sb, half(h))))
            for c in range(h * HALF // PIECE, (h + 1) * HALF // PIECE):
                cols = slice(c * PIECE, (c + 1) * PIECE)
                logits = bank("logits%d" % c)
                product(logits[:, :PIECE], w3_mx, cols)
                nc.scalar.activation(a[:, cols], logits[:, :PIECE], ACT.Exp, bias=zero[:])

        w2_mx = quantize("w2", w2_grouped)
        w1_grouped = interleave(place("w1_grouped", [P, N, PACK], BF16, 1024), w1_raw, nc.vector.tensor_copy)
        r = [bank("r%d" % h) for h in range(S // HALF)]
        for h in range(S // HALF):
            product(r[h][:, :HALF], w2_mx, half(h))
        w1_mx = quantize("w1", w1_grouped, "w2_grouped")
        y = [bank(name) for name in ("y0", "y1")]
        for h in range(S // HALF):
            product(y[h][:, :HALF], w1_mx, half(h))

        rr = sb("rr", [P, S], F32, "w3_raw")
        nc.vector.tensor_scalar_max(rr[:, half(0)], r[0][:, :HALF], 0.0)
        nc.scalar.activation(rr[:, half(1)], r[1][:, :HALF], ACT.Relu)
        a0 = [place("a0_0", [P, WIDTH], F32, 1536), place("a0_1", [P, WIDTH], F32, 1024)]
        nc.vector.tensor_copy(a0[0][:], at(a, 0, block(0)))
        nc.scalar.activation(a0[1][:], at(a, 0, block(1)), ACT.Copy)
        rr_at = [sb("rr_at0", [P, V], F32), place("rr_at1", [P, V], F32, 1792), place("rr_at2", [P, V], F32, 768)]
        nc.scalar.activation(rr_at[0][:], at(rr, 0, every), ACT.Copy)
        ya = sb("ya", [P, S], F32)
        for h in range(S // HALF):
            nc.vector.tensor_tensor(ya[:, half(h)], y[h][:, :HALF], a[:, half(h)], ALU.mult)
        num0 = sb("num0", [P, V], F32)
        nc.scalar.activation(num0[:], at(ya, 0, every), ACT.Copy)
        a01 = sb("a01", [P, V], F32)
        for b in range(BLOCKS):
            nc.vector.tensor_tensor(a01[:, block(b)], at(a, 1, block(b)), a0[b][:], ALU.add)
        for i in range(1, LISTS):
            nc.scalar.activation(rr_at[i][:], at(rr, i, every), ACT.Copy)
        den = sb("den", [P, V], F32)
        for b in range(BLOCKS):
            nc.vector.tensor_tensor(den[:, block(b)], at(a, 2, block(b)), a01[:, block(b)], ALU.add)
        num01 = sb("num01", [P, V], F32)
        nc.vector.tensor_tensor(num01[:], at(ya, 1, every), num0[:], ALU.add)
        pt_den = sb("pt_den", [P, V], F32)
        nc.vector.tensor_tensor(pt_den[:], pt_sb[:], den[:], ALU.mult)
        off01 = sb("off01", [P, V], F32, "a01")
        nc.vector.tensor_tensor(off01[:], rr_at[0][:], rr_at[1][:], ALU.min)
        gap01 = sb("gap01", [P, V], F32)
        nc.vector.tensor_tensor(gap01[:], num01[:], pt_den[:], ALU.subtract)
        off = sb("off", [P, V], F32)
        nc.vector.tensor_tensor(off[:], off01[:], rr_at[2][:], ALU.min)

        root = sb("root", [P, V], F32, "w3_raw")
        for b in range(BLOCKS):
            nc.scalar.activation(root[:, block(b)], den[:, block(b)], ACT.Abs_reciprocal_sqrt)

        gap = fetch_with("gap", ya, 2, [gap01[:, block(b)] for b in range(BLOCKS)], ALU.add)
        rec = blocks("rec")
        for b in range(BLOCKS):
            nc.scalar.activation(rec[b][:], root[:, block(b)], ACT.Square)

        size = blocks("size")
        off_den = sb("off_den", [P, V], F32, "num01")
        for b in range(BLOCKS):
            nc.vector.scalar_tensor_tensor(size[b][:], gap[b], -1.0, gap[b], ALU.mult, ALU.max)
            nc.vector.tensor_tensor(off_den[:, block(b)], off[:, block(b)], den[:, block(b)], ALU.mult)
        beyond = blocks("beyond")
        for b in range(BLOCKS):
            nc.vector.tensor_tensor(beyond[b][:], size[b][:], off_den[:, block(b)], ALU.subtract)
        result = sb("result", [P, V], F32, "gap1")
        for b in range(BLOCKS):
            nc.vector.scalar_tensor_tensor(result[:, block(b)], beyond[b][:], 0.0, rec[b][:], ALU.max, ALU.mult)
        nc.sync.dma_start(out, result[:])
